import numpy as np, ml_dtypes
CORES = [6,15,38,47]
N = 4
import mx_ref
BF = ml_dtypes.bfloat16
def gentries(a):
    return np.ascontiguousarray(a.reshape(8, 16, -1).transpose(0, 2, 1)).reshape(8, -1)
def gtable(e):
    e = np.asarray(e); return np.ascontiguousarray(e.reshape(8, -1, 16).transpose(0, 2, 1)).reshape(128, -1).astype(np.int32)
def gcols(t, e):
    v = np.concatenate([t.reshape(8, 16, -1, 4), np.zeros((8, 16, 1, 4), BF)], axis=2)
    return np.ascontiguousarray(np.stack([v[g][:, e[g]] for g in range(8)])).reshape(128, -1)
def tile(rs):
    return np.stack(rs, axis=2).reshape(128, -1).astype(BF)
def pick(q, e):
    c = np.concatenate([q[0].reshape(128, -1, 4), np.zeros((128, 1, 4), np.uint8)], axis=1); s = np.concatenate([q[1], np.ones((16, 1), np.uint8)], axis=1)
    return (np.ascontiguousarray(c[:, e].reshape(128, -1)), np.ascontiguousarray(s[:, e]))
def join(*qs):
    return (np.concatenate([q[0] for q in qs], axis=1), np.concatenate([q[1] for q in qs], axis=1))
def put(q, e, v):
    c, s = q[0].reshape(128, -1, 4).copy(), q[1].copy(); c[:, e] = v[0].reshape(128, -1, 4); s[:, e] = v[1]
    return (c.reshape(128, -1), s)
def pk(c, s):
    return (np.ascontiguousarray(c), mx_ref.live(s))
def emit(q):
    return q[0], q[1]
def packed(v, rng):
    q = [mx_ref.quantize(np.ascontiguousarray(v[r])) for r in range(N)]
    return np.stack([a for a, b in q]), np.stack([mx_ref.plane(b, rng) for a, b in q])
def values_of_codes():
    e, c = np.zeros((128, 128, 4), np.float32), np.zeros((128, 2, 4), np.uint8)
    e[np.arange(128), np.arange(128), 0] = 1
    c[:127, :, 0] = np.arange(256).reshape(2, 128).T[:127]
    return mx_ref.matmul(mx_ref.quantize(e.reshape(128, 512).astype(BF)), (c.reshape(128, 8), np.full((16, 2), 127, np.uint8))).T.reshape(-1).astype(np.float64)
CODE_VALUE, SCALE_VALUE = values_of_codes(), 2.0 ** (np.arange(256) - 127.0)
def decode(q):
    return (CODE_VALUE[q[0]].reshape(16, 8, -1, 4) * SCALE_VALUE[q[1]][:, None, :, None] + 0.0).reshape(128, -1).astype(np.float32)
def f(rng, *shape):
    return mx_ref.flush((rng.standard_normal(shape, dtype=np.float32) * np.exp2(rng.integers(-2, 3, shape[:-1] + (1,)))).astype(BF))
def wide(rng, *shape, cols=0):
    v = rng.standard_normal(shape, dtype=np.float32) * np.exp2(rng.integers(-12, 13, shape)).astype(np.float32)
    if cols: v *= np.repeat(np.exp2(rng.integers(-cols, cols + 1, shape[:-2] + (1, shape[-1] // 4))) * (rng.random(shape[:-2] + (1, shape[-1] // 4)) > 0.0625), 4, axis=-1).astype(np.float32)
    return mx_ref.flush(v.astype(BF))
C, J = 320, 128
STEP = [1, 2, 3]
def big(v):
    v = v.astype(np.float32)
    v[np.abs(v) < np.float32(2.0 ** -12)] = 0
    return v.astype(BF)
def numbers_of(rng):
    return {"x": big(f(rng, N, 128, 4 * C)), "u": np.array(f(rng, N, 128, 512)), "v": np.array(f(rng, N, 128, 512))}
def maps_of(rng):
    return rng.permuted(np.tile(np.arange(C), (N, 8, 1)), axis=2)
def arrivals(rng, m, right=0.75):
    return np.where(rng.random((N, 8, 4, C)) < right, m[:, :, None], rng.integers(0, C, (N, 8, 4, C)))
def lists(m, a):
    return {"mp": np.stack([gtable(m[r]) for r in range(N)]), "ar": np.stack([gtable(a[r].reshape(8, 4 * C)) for r in range(N)])}
def layers(rng):
    return big(f(rng, N, 128, 2048)).reshape(N, 128, 4, 128, 4)
def weights(rng, w):
    c, s = packed(np.ascontiguousarray(w).reshape(N, 128, 2048), rng)
    return {"wc": c, "ws": s}
def setup_inputs(rng):
    m = maps_of(rng)
    return {**numbers_of(rng), **lists(m, arrivals(rng, m)), **weights(rng, layers(rng))}
def setup_inputs_ties(rng):
    d = numbers_of(rng)
    o = rng.permutation(N)
    x = d["x"].reshape(N, 128, C, 4)
    x[:, :8, :, :2] = rng.integers(0, 3, (N, 8, C, 2)).astype(np.float32).astype(BF)
    x[:, 8:16, :, :2] = 1
    x[o[0], :16, :, :2] = 0
    u = d["u"].reshape(N, 128, 128, 4)
    u[:, :, ::16] = 0
    u[:, :, 1::16] = 0
    w = layers(rng)
    for e in range(2):
        for p in range(16):
            w[:, :, e, p] = 0
            w[:, p, e, p, e] = 32
        for g in range(8):
            for h in range(0, 16, 8):
                w[:, :, e, 16 * g + h] = 0
                w[:, g + h, e, 16 * g + h, e] = 32
                u[:, 16 * g + h, 16 * g + e, e] = 1.0 if h == 0 else -1.0
    m = maps_of(rng)
    for r in range(N): m[r, 1:] = rng.permutation(C)[:8][rng.integers(0, 8, (7, C))]
    one = int(o[1])
    goal = int(m[one, 1, 0])
    m[one, 1] = goal
    right = np.array([1.0, 0.75] + [0.25] * 6)[:, None, None]
    a = arrivals(rng, m, right)
    a[one, 1] = m[one, 1]
    a[one, 2, :, goal] = (m[one, 2, goal] + 1 + np.arange(4)) % C
    x[one, 2, m[one, 0, :J], :2] = 0
    x[one, 2, m[one, 0, 0], :2] = 2
    return {"x": x.reshape(N, 128, 4 * C), "u": u.reshape(N, 128, 512), "v": d["v"], **lists(m, a), **weights(rng, w)}
def setup_inputs_near(rng):
    d = numbers_of(rng)
    x = d["x"].reshape(N, 128, C, 4)
    x.reshape(N, 8, 16, C, 4)[:, :, 8:] = 1
    u = d["u"].reshape(N, 128, 128, 4)
    u[:, :, ::16] = 0
    u[:, :, 1::16] = 0
    o = rng.permutation(N) % 4
    m = maps_of(rng)
    for r in range(N):
        t = np.array([[9.0, 8.0], [11.0, 10.0], [10.0, 9.0]])[rng.integers(0, 3, (8, C, 2))].reshape(8, C, 4) * 0.125
        far = m[r, 0, rng.permutation(J)[:12]]
        if o[r] % 2 == 0: t = t * 2.0 ** -12
        if o[r] < 2:
            t[:, far[:8]] *= 2.0 ** 25 if o[r] == 0 else 2.0 ** 13
            x[r, 15] = 0
            x[r, 15, far[8:], 0] = 1
        x[r, :8] = t.astype(np.float32).astype(BF)
        k = 2.0 ** -30 if o[r] % 2 == 0 else 1.0
        for h in range(0, 128, 16):
            for b in range(2):
                u[r, h + 8 + 2 * b, h + b, 0] = 1.125 * k
                u[r, h + 9 + 2 * b, h + b, 0] = -1.25 * k
                if o[r] < 2: u[r, 16, h + b, 0] = 2.0 ** 30
    w = layers(rng)
    w.reshape(N, 128, 4, 8, 16, 4)[:, :, :, :, 8:] = 0
    w[:, :, :, :8] = 0
    w[:, :, 0, 16] = 0
    w[:, 15, 0, 16, 0] = 32
    for g in range(8):
        for i in range(4):
            w[:, g, i, g, i] = 32
            w[:, g, 0, 16 * g + 8 + i, i] = 2.0 ** -13
    return {"x": x.reshape(N, 128, 4 * C), "u": u.reshape(N, 128, 512), "v": d["v"], **lists(m, arrivals(rng, m)), **weights(rng, w)}
def setup_inputs_ends(rng):
    o = rng.permutation(N) % 4
    x = rng.choice([-1.0, 1.0], (N, 128, 4 * C))
    u = rng.choice([-1.0, 1.0], (N, 128, 128, 4))
    v = rng.choice([-1.0, 1.0], (N, 128, 512))
    m, a = np.zeros((N, 8, C), int), np.full((N, 8, 4, C), C - 1)
    for r in range(N):
        if o[r] == 0:
            x[r] = 1.0
            u[r] = u[r, :1, :, :1].copy()
        if o[r] % 2 == 0: m[r] = C - 1
        if o[r] == 2: a[r, :, ::3] = 0
        if o[r] == 3:
            x[r] = -1.0
            m[r] = np.arange(C)
            a[r] = np.arange(C)[::-1]
        x[r] *= 2.0 ** -12 if o[r] == 2 else 2.0 ** 14
        u[r] *= 2.0 ** -30 if o[r] == 2 else 2.0 ** 30
        v[r] *= 2.0 ** -30 if o[r] == 2 else 2.0 ** 30
    w = np.full((N, 128, 4, 128, 4), 4.0)
    w[:, :, :3, :, :2] = 8.0
    w[:, :, :3, :, 2:] = 0.0
    w[:, :, 3] *= rng.choice([-1.0, 1.0], (N, 128, 128, 4))
    return {"x": x.astype(BF), "u": u.reshape(N, 128, 512).astype(BF), "v": v.astype(BF), **lists(m, a), **weights(rng, w.astype(BF))}
def setup_inputs_blocks(rng):
    d = numbers_of(rng)
    s = (1.0 + (2 * rng.integers(0, 64, (N, 16, 8, C, 4)) + 1) * 2.0 ** -7) * np.exp2(-rng.integers(8, 15, (N, 16, 8, C, 4)).astype(np.float64))
    top = np.arange(32).reshape(8, 1, 4) == rng.integers(0, 32, (N, 16, C))[:, :, None, :, None]
    x = np.where(top, 1.96875, s) * rng.choice([-1.0, 1.0], (N, 16, 8, C, 4)) * np.exp2(rng.integers(2, 8, (N, 16, 1, C, 1)).astype(np.float64))
    m = maps_of(rng)
    return {"x": x.reshape(N, 128, 4 * C).astype(np.float32).astype(BF), "u": d["u"], "v": d["v"], **lists(m, arrivals(rng, m)), **weights(rng, layers(rng))}
def setup_inputs_spread(rng):
    d = setup_inputs(rng)
    d["x"] = big(wide(rng, N, 128, 4 * C, cols=4).astype(np.float32) * np.float32(2.0 ** -5))
    return d
def check_inputs(d):
    b = []
    for k, lo, hi in (("x", 2.0 ** -12, 2.0 ** 14), ("u", 2.0 ** -30, 2.0 ** 30), ("v", 2.0 ** -30, 2.0 ** 30)):
        a = np.abs(d[k].astype(np.float32))
        if not (np.isfinite(a).all() and ((a == 0) | (a >= lo) & (a <= hi)).all()): b.append("a value of " + k)
    for k in ("mp", "ar"):
        if not ((d[k] >= 0) & (d[k] < C)).all(): b.append("an entry of " + k)
    none, least, most = [emit(mx_ref.quantize(np.full((128, 16), k, np.float32).astype(BF)))[1][0, 0] for k in (0.0, 2.0 ** -30, 2.0 ** 30)]
    for r in range(N):
        if ((d["wc"][r] == 0x7F) | (d["wc"][r] == 0xFF)).any(): b.append("wc: a code that is no number")
        s = mx_ref.live(d["ws"][r])
        if ((s != none) & ((s < least) | (s > most))).any(): b.append("ws: a scale out of range")
        else:
            a = np.abs(decode(pk(d["wc"][r], d["ws"][r]))).reshape(128, 512, 4)
            if (np.sum(a, axis=(0, 2), dtype=np.float64) > 2048).any(): b.append("a column of W")
    return b
def chains(m):
    e = [np.arange(J)]
    for g in range(8): e.append(m[g, e[g]])
    return np.stack(e[:8]), np.stack(e[1:])
def reference(x, u, v, mp, ar, wc, ws):
    qu = [mx_ref.quantize(u[r]) for r in range(N)]
    lay = [pk(wc[r], ws[r]) for r in range(N)]
    now = [x[r] for r in range(N)]
    maps = np.stack([gentries(mp[r]) for r in range(N)])
    cand = np.stack([gentries(ar[r]).reshape(8, 4, C) for r in range(N)])
    grp = np.arange(8)
    for h in STEP:
        for r in range(N):
            donor = (r + h) % N
            old = decode(mx_ref.quantize(now[r])).astype(BF)
            e, l = chains(maps[r])
            m = mx_ref.quantize(gcols(old, l))
            q = mx_ref.quantize(tile([np.maximum(mx_ref.matmul(pick(lay[donor], np.arange(128 * b, 128 * b + 128)), m), np.float32(0.0)) * np.float32(0.03125) for b in range(4)]))
            s = mx_ref.matmul(qu[r], q)
            a = cand[r][grp[:, None], 2 * (s[::16] > 0) + (s[1::16] > 0), e]
            wrong = a != l
            first = np.argmax(wrong, axis=0)
            for j in range(J - 1, -1, -1):
                g = first[j]
                if wrong[g, j]: maps[r, g, e[g, j]] = a[g, j]
            l = chains(maps[r])[1]
            n = np.tile(J + np.arange(C), (8, 1))
            for j in range(J - 1, -1, -1): n[grp, l[:, j]] = j
            other = gcols(np.concatenate([decode(q).astype(BF), old], axis=1), n)
            now[r] = ((old.astype(np.float32) + other.astype(np.float32)) * np.float32(0.5)).astype(BF)
    y, fo = np.zeros((N, 128, C), np.float32), np.zeros((N, 8, C), np.float32)
    oc, osc = np.zeros((N, 128, 4 * C), np.uint8), np.zeros((N, 16, C), np.uint8)
    for r in range(N):
        q = mx_ref.quantize(now[r])
        y[r] = mx_ref.matmul(mx_ref.quantize(v[r]), q)
        fo[r] = maps[r]
        oc[r], osc[r] = emit(q)
    return {"y": y, "fo": fo, "oc": oc, "osc": osc}

@@ -1,0 +1,492 @@
+from concourse.mybir import dt, AluOpType as Op, AxisListType, ActivationFunctionType as Act
+
+F32, BF, I32, U16, MXC, U8 = "float32", "bfloat16", "int32", "uint16", "float8_e4m3fn_x4", "uint8"
+SCRATCH = {
+    "xi": ("sbuf", [128, 1280], BF), "ui": ("sbuf", [128, 512], BF), "vi": ("sbuf", [128, 512], BF),
+    "mwi": ("sbuf", [128, 192], I32), "mwf": ("sbuf", [128, 192], F32),
+    "cwi": ("sbuf", [128, 1280], I32), "cwf": ("sbuf", [128, 1280], F32),
+    "wcs": ("sbuf", [128, 512], MXC), "wps": ("sbuf", [128, 512], U8),
+    "wdc": ("sbuf", [128, 512], MXC), "wdp": ("sbuf", [128, 512], U8),
+    "pi": ("sbuf", [128, 16], I32), "pf": ("sbuf", [128, 32], F32), "nat": ("sbuf", [128, 320], F32), "nat512": ("sbuf", [128, 320], F32),
+    "ci": ("sbuf", [128, 160], I32), "cj": ("sbuf", [128, 160], I32), "cf": ("sbuf", [128, 192], F32),
+    "tril": ("sbuf", [128, 128], F32), "idb": ("sbuf", [128, 128], BF), "mod": ("sbuf", [128, 128], BF), "m8": ("sbuf", [128, 8], BF),
+    "l0": ("sbuf", [128, 4], U16), "lr": ("sbuf", [128, 8], U16), "ly": ("sbuf", [128, 20], U16), "pk": ("sbuf", [128, 4], U16),
+    "la": ("sbuf", [128, 4], U16),
+    "zt": ("sbuf", [128, 512], BF), "ce": ("sbuf", [128, 2048], BF), "ca": ("sbuf", [128, 1536], BF), "cb": ("sbuf", [128, 1536], BF),
+    "qe": ("sbuf", [128, 512], MXC), "se": ("sbuf", [128, 512], U8),
+    "qa": ("sbuf", [128, 384], MXC), "sa": ("sbuf", [128, 384], U8),
+    "qb": ("sbuf", [128, 384], MXC), "sb": ("sbuf", [128, 384], U8),
+    "qu": ("sbuf", [128, 128], MXC), "su": ("sbuf", [128, 128], U8),
+    "qv": ("sbuf", [128, 128], MXC), "sv": ("sbuf", [128, 128], U8),
+    "fs": ("sbuf", [128, 192], F32),
+    "yb": ("sbuf", [128, 2560], F32), "fw": ("sbuf", [128, 2880], F32),
+    "ox": ("sbuf", [128, 576], F32), "tt": ("sbuf", [128, 448], F32), "of": ("sbuf", [128, 32], U16),
+    "rl": ("sbuf", [128, 128], F32), "tl": ("sbuf", [128, 128], F32), "lw": ("sbuf", [128, 16], U16),
+    "rle": ("sbuf", [128, 128], F32), "te": ("sbuf", [128, 128], F32), "ew": ("sbuf", [128, 16], I32),
+    "e1": ("sbuf", [128, 8], I32), "e2": ("sbuf", [128, 8], I32), "ec": ("sbuf", [128, 8], I32), "el": ("sbuf", [128, 8], U16), "lc": ("sbuf", [128, 32], U16),
+    "rf": ("sbuf", [128, 768], F32), "cp": ("sbuf", [128, 48], F32),
+    "ne": ("sbuf", [128, 32], F32), "sk": ("sbuf", [128, 32], F32), "pp": ("sbuf", [128, 32], F32),
+    "kk": ("sbuf", [128, 128], F32), "dd": ("sbuf", [128, 1024], F32), "fl": ("sbuf", [128, 8], U16),
+    "sg": ("sbuf", [128, 256], F32), "xx": ("sbuf", [128, 32], F32), "yy": ("sbuf", [128, 36], F32),
+    "qd": ("sbuf", [128, 8], I32),
+    "b1": ("sbuf", [128, 1536], BF), "b2": ("sbuf", [128, 512], BF),
+    "qk": ("sbuf", [128, 384], MXC), "sk1": ("sbuf", [128, 384], U8), "ql": ("sbuf", [128, 128], MXC), "sl": ("sbuf", [128, 128], U8),
+    "kt": ("sbuf", [128, 128], F32), "eq": ("sbuf", [128, 128], F32), "ofs": ("sbuf", [128, 8], U16),
+    "va": ("sbuf", [128, 128], F32),
+    "fh": ("sbuf", [128, 1280], BF), "dh": ("sbuf", [128, 512], BF), "fg": ("sbuf", [128, 512], F32),
+    "nt": ("sbuf", [128, 512], BF), "qn": ("sbuf", [128, 128], MXC), "sn": ("sbuf", [128, 128], U8),
+    "mt": ("sbuf", [128, 512], BF), "ht": ("sbuf", [128, 512], BF),
+    "xt": ("sbuf", [128, 1792], BF), "qx": ("sbuf", [128, 320], MXC), "sx": ("sbuf", [128, 320], U8),
+    "xl": ("sbuf", [128, 32], U16), "yo": ("sbuf", [128, 320], F32),
+}
+for _r in range(3):
+    SCRATCH["qm%d" % _r] = ("sbuf", [128, 128], MXC)
+    SCRATCH["sm%d" % _r] = ("sbuf", [128, 128], U8)
+    SCRATCH["qh%d" % _r] = ("sbuf", [128, 128], MXC)
+    SCRATCH["sh%d" % _r] = ("sbuf", [128, 128], U8)
+    if _r < 2:
+        SCRATCH["mc%d" % _r] = ("sbuf", [128, 128], MXC)
+        SCRATCH["mp_%d" % _r] = ("sbuf", [128, 128], U8)
+        SCRATCH["hc%d" % _r] = ("sbuf", [128, 128], MXC)
+        SCRATCH["hp%d" % _r] = ("sbuf", [128, 128], U8)
+for _r in range(8):
+    SCRATCH["p%d" % _r] = ("psum", [128, 512], F32)
+SMALL = {n: 8 * k for k, n in enumerate(("jw", "jd", "sc", "nq", "dg", "kf", "lo", "kw", "dj", "t1", "t2", "rq", "fi", "wn", "xd", "nl"))}
+SEMAPHORES = ["v", "s", "t", "p", "dx", "du", "dv", "dw", "da", "dc", "do", "aw", "am0", "am1", "ah0", "ah1", "ls"] + ["dm%d" % _r for _r in range(8)]
+STEP = [1, 2, 3]
+
+
+def rank_program(g, core, T, topo):
+    r = T.rank_of(core)
+    if r is None:
+        return
+    N = len(T.cores)
+    Q = {"v": g.vector, "s": g.scalar, "t": g.tensor, "p": g, "y": g.sync}
+    known = {q: {} for q in Q}
+    tot, wr, rd = {}, {}, {}
+
+    def gate(q, reads, writes, acc=False):
+        toks = []
+        for k in reads:
+            toks += wr.get(k, [])
+            if k[0] == "#":
+                toks += [t for t in rd.get(k, []) if t[3] != q]
+        for k in writes:
+            if not acc:
+                toks += wr.get(k, [])
+            toks += rd.get(k, [])
+        want = {}
+        for sem, val, snap, _ in toks:
+            if isinstance(val, tuple):
+                val = val[0] if known[q].get(sem, 0) >= val[0] else tot[sem]
+            if val > want.get(sem, (0, None))[0]:
+                want[sem] = (val, snap)
+        for sem in sorted(want, key=lambda m: -len(want[m][1])):
+            val, snap = want[sem]
+            if known[q].get(sem, 0) < val:
+                Q[q].wait_ge(T.sem[sem], val)
+                known[q][sem] = val
+                for a, b in snap.items():
+                    known[q][a] = max(known[q].get(a, 0), b)
+
+    def note(tok, reads, writes):
+        for k in reads:
+            rd.setdefault(k, []).append(tok)
+        for k in writes:
+            wr[k] = [tok]
+            rd[k] = []
+
+    def op(q, call, reads, writes, acc=False):
+        gate(q, reads, writes, acc)
+        tot[q] = tot.get(q, 0) + 1
+        call().then_inc(T.sem[q], 1)
+        note((q, tot[q], dict(known[q]), q), reads, writes)
+
+    def dma(q, sem, out, in_, reads, writes):
+        gate(q, reads, writes)
+        tot[sem] = tot.get(sem, 0) + 16
+        Q[q].dma_start(out, in_).then_inc(T.sem[sem], 16)
+        note((sem, (tot[sem],), dict(known[q]), sem), reads, writes)
+
+    def send(pairs, dst, sem, reads):
+        gate("p", reads, [])
+        rid, pid, _ = topo.addr(dst)
+        mask = topo.mask(core, dst)
+        for out, in_ in pairs:
+            g.remote_dma(out, in_, T.sem[sem], T.sem.ls, pid, rid, mask)
+            tot["ls"] = tot.get("ls", 0) + len(topo.engines(core, dst))
+
+    def arrives(sem, src, writes):
+        tot[sem] = 2 * len(topo.engines(src, core))
+        for k in writes:
+            wr[k] = [(sem, tot[sem], {}, sem)]
+
+    V, S = g.vector, g.scalar
+    B8 = dt.uint8
+
+    def ts(q_out, in0, s1, op0, reads, writes, s2=None, op1=None):
+        if op1 is None:
+            op("v", lambda: V.tensor_scalar(q_out, in0, s1, None, op0), reads, writes)
+        else:
+            op("v", lambda: V.tensor_scalar(q_out, in0, s1, s2, op0, op1), reads, writes)
+
+    def tt(out, a, b, o, reads, writes):
+        op("v", lambda: V.tensor_tensor(out, a, b, o), reads, writes)
+
+    def cp(out, in_, reads, writes):
+        op("v", lambda: V.tensor_copy(out, in_), reads, writes)
+
+    def tr(out, in_, reads, writes):
+        op("v", lambda: V.transpose(out, in_), reads, writes)
+
+    def act(out, in_, reads, writes, func=Act.Copy, **kw):
+        op("s", lambda: S.activation(out, in_, func, **kw), reads, writes)
+
+    def red(out, in_, o, reads, writes, **kw):
+        op("v", lambda: V.tensor_reduce(out, in_, AxisListType.X, o, **kw), reads, writes)
+
+    def fill(ap, val, writes):
+        op("v", lambda: V.memset(ap, val), [], writes)
+
+    def quant(q, s, t, reads, writes):
+        op("v", lambda: V.quantize_mx(q, s, t), reads, writes)
+
+    def mm(out, l, ls, m, ms, reads, writes, start=True, stop=True):
+        op("t", lambda: g.tensor.matmul_mx(out, l, ls, m, ms, start, stop), reads, writes, acc=not start)
+
+    def iota(out, pattern, base, cm, writes, flt):
+        if flt:
+            op("p", lambda: g.iota(out, pattern, base, cm, allow_small_or_imprecise_dtypes=True), [], writes)
+        else:
+            op("p", lambda: g.iota(out, pattern, base, cm), [], writes)
+
+    def sm(name, n=8):
+        return T.fs[:, SMALL[name]:SMALL[name] + n]
+
+    PS = [T["p%d" % k] for k in range(8)]
+    M4 = ["M%d" % t for t in range(4)]
+    H4 = ["H%d" % t for t in range(4)]
+    N4 = ["N%d" % t for t in range(4)]
+    X4 = ["X%d" % t for t in range(4)]
+    PI, PF = T.pi, T.pf
+    pf = lambda k: PF[:, k:k + 1]
+
+    for m in range(8):
+        for q in range(8):
+            dma("ys"[q % 2], "dm%d" % m, T.mwi[16 * q:16 * q + 16, 24 * m:24 * m + 20], T.mp[16 * m:16 * m + 16, :], [], ["mwi%d.%d" % (m, q)])
+        if m == 1:
+            dma("y", "dx", T.xi[:], T.x[:], [], ["xi"])
+    dma("y", "dw", T.wcs[:].bitcast(B8), T.wc[:], [], ["wcs"])
+    dma("y", "dw", T.wps[:], T.ws[:], [], ["wps"])
+    for i in range(16):
+        dma("y", "da", T.cwi[i:128:16, :], T.ar[:], [], ["cwi%d" % i])
+    dma("y", "du", T.ui[:], T.u[:], [], ["ui"])
+    dma("y", "dv", T.vi[:], T.v[:], [], ["vi"])
+
+    iota(PI[:, 9:10], [[0, 1]], 0, 1, ["pi9"], False)
+    iota(T.cf[:, 0:20], [[2, 10], [0, 2]], 0, 0, ["cf0"], True)
+    iota(T.cf[:, 32:40], [[16, 4], [64, 2]], 0, 0, ["cf1"], True)
+    iota(T.cf[:, 64:128], [[32, 2], [64, 2], [1, 16]], 0, 0, ["cf4"], True)
+    iota(T.nat[:], [[1, 320]], 0, 0, ["nat"], True)
+    iota(T.zt[:], [[0, 512]], 0, 0, ["zt"], True)
+    for b in range(4):
+        op("p", lambda b=b: g.affine_select(T.ce[:, 512 * b:512 * b + 512], T.zt[:], [[-1, 512]], Op.not_equal, 1.0, b, 4), ["zt"], ["ce%d" % b])
+    iota(T.ci[:, 0:128], [[-1, 128]], 128, 1, ["cia"], False)
+    iota(T.ci[:, 128:136], [[-16, 8]], 0, 1, ["cib"], False)
+    iota(T.cf[:, 56:58], [[-128, 2]], 128, 0, ["cf3"], True)
+    for col, sh, an in ((0, 0, 15), (1, 4, 1), (2, 5, 3), (4, 0, 1), (5, 1, 1), (6, 2, 1), (7, 0, 7), (8, 3, 1)):
+        ts(PI[:, col:col + 1], PI[:, 9:10], sh, Op.logical_shift_right, ["pi9"], ["pi%d" % col], an, Op.bitwise_and)
+    ts(PI[:, 3:4], PI[:, 9:10], 4, Op.logical_shift_right, ["pi9"], ["pi3"])
+    cp(PF[:, 0:10], PI[:, 0:10], ["pi%d" % k for k in range(10)], ["pf"])
+    fill(T.b2[:], 0.0, ["b2"])
+    ts(T.ly[:], T.cf[:, 0:20], pf(1), Op.add, ["cf0", "pf"], ["ly"])
+    ts(pf(10), pf(1), 64.0, Op.mult, ["pf"], ["pf10"], pf(0), Op.add)
+    ts(pf(11), pf(1), 16.0, Op.mult, ["pf"], ["pf11"])
+    ts(pf(12), pf(2), 128.0, Op.mult, ["pf"], ["pf12"], pf(0), Op.add)
+    tt(pf(13), pf(6), pf(4), Op.subtract, ["pf"], ["pf13"])
+    ts(pf(15), pf(5), 4.0, Op.mult, ["pf"], ["pf15"], pf(4), Op.add)
+    tt(pf(14), pf(13), pf(1), Op.mult, ["pf13", "pf"], ["pf14"])
+    tt(pf(16), pf(15), pf(6), Op.add, ["pf15", "pf"], ["pf16"])
+    ts(T.lr[:], T.cf[:, 32:40], pf(12), Op.add, ["cf1", "pf12"], ["lr"])
+    ts(pf(17), pf(16), pf(4), Op.add, ["pf16", "pf"], ["pf17"], pf(14), Op.add)
+    ts(pf(18), pf(16), pf(6), Op.add, ["pf16", "pf"], ["pf18"], pf(14), Op.subtract)
+    ts(T.ox[:, 0:64], T.cf[:, 64:128], pf(11), Op.add, ["cf4", "pf11"], ["ox0"])
+    ts(T.pk[:, 0:1], pf(17), 16.0, Op.mult, ["pf17"], ["pk0"])
+    ts(T.pk[:, 2:3], pf(18), 16.0, Op.mult, ["pf18"], ["pk1"])
+    ts(T.l0[:], T.nat[:, 0:4], 16.0, Op.mult, ["nat", "pf10"], ["l0"], pf(10), Op.add)
+    fill(T.b1[:], 0.0, ["b1"])
+    fill(T.ca[:], 0.0, ["ca"])
+
+    def step_a(s):
+        lst, key = (T.l0[:], "l0") if s == 0 else (T.of[:, 4 * s - 4:4 * s], "of%d" % (s - 1))
+        cp(T.ox[:, 64 * s + 64:64 * s + 128], T.fw[:, 320 * (8 - s):320 * (8 - s) + 320].indirect(lst), ["fw%d" % s, key], ["ox%d" % (s + 1)])
+
+    def step_b(s):
+        tr(T.tt[:, 64 * s:64 * s + 64], T.ox[:, 64 * s + 64:64 * s + 128], ["ox%d" % (s + 1)], ["tt%d" % s])
+
+    def step_c(s):
+        cp(T.of[:, 4 * s:4 * s + 4], T.tt[:, 64 * s:64 * s + 64:16], ["tt%d" % s], ["of%d" % s])
+
+    FWALL = ["fw%d" % s for s in range(8)]
+
+    def places():
+        cp(T.rl[:], T.ox[:, 64:576].indirect(T.lr[:]), ["ox%d" % k for k in range(1, 9)] + ["lr"], ["rl"])
+        tr(T.tl[:], T.rl[:], ["rl"], ["tl"])
+        cp(T.lw[:], T.tl[:].indirect(T.pk[:, 0:1]), ["tl", "pk0"], ["lw"])
+
+    def decode_x():
+        for t in range(4):
+            mm(PS[t][:, 0:320], T.qe[:, 128 * t:128 * t + 128], T.se[:, 128 * t:128 * t + 128], T.qx[:], T.sx[:], ["qe", "qx"], ["#%d" % t])
+        for t in range(4):
+            act(T.fh[:, 320 * t:320 * t + 320], PS[t][:, 0:320], ["#%d" % t], ["fh%d" % t], scale=0.5)
+
+    def base_x():
+        for t in range(4):
+            act(T.xt[:, t:1280:4], T.fh[:, 320 * t:320 * t + 320], ["fh%d" % t], [X4[t]], scale=2.0)
+
+    def spread(m):
+        act(T.yb[:, 320 * m:320 * m + 320], T.mwf[:, 24 * m:24 * m + 20].indirect(T.ly[:]), ["mwf%d" % m, "ly"], ["yb%d" % m])
+
+    def turn(m):
+        tr(T.fw[:, 320 * (8 - m):320 * (8 - m) + 320], T.yb[:, 320 * m:320 * m + 320], ["yb%d" % m], ["fw%d" % m])
+
+    def unpack(m):
+        cp(T.mwf[:, 24 * m:24 * m + 20], T.mwi[:, 24 * m:24 * m + 20], ["mwi%d.%d" % (m, q) for q in range(8)], ["mwf%d" % m])
+
+    unpack(0)
+    spread(0)
+    unpack(1)
+    spread(1)
+    unpack(2)
+    spread(2)
+    turn(0)
+    step_a(0)
+    turn(1)
+    for s in range(7):
+        step_b(s)
+        if s + 3 < 8:
+            unpack(s + 3)
+            spread(s + 3)
+        step_c(s)
+        if s == 1:
+            fill(T.cb[:], 0.0, ["cb"])
+        elif s == 2:
+            quant(T.qx[:], T.sx[:], T.xi[:], ["xi"], ["qx"])
+        elif s == 3:
+            quant(T.qe[:], T.se[:], T.ce[:], ["ce%d" % t for t in range(4)], ["qe"])
+        elif s == 4:
+            decode_x()
+        step_a(s + 1)
+        if s + 2 < 8:
+            turn(s + 2)
+    places()
+
+    def more_constants():
+        ts(T.idb[:], T.ci[:, 0:128], 128.0, Op.is_equal, ["cia"], ["idb"])
+        for t in range(5):
+            fill(T.fs[:, SMALL["sc"] + t:SMALL["sc"] + t + 1], 32.0 ** -t, ["sc%d" % t])
+        fill(T.fs[:, SMALL["sc"] + 5:SMALL["sc"] + 6], 0.0, ["sc5"])
+        ts(T.cj[:, 0:128], T.ci[:, 0:128], 15, Op.bitwise_and, ["cia"], ["cja"])
+        ts(T.cj[:, 128:136], T.ci[:, 128:136], 4, Op.arith_shift_right, ["cib"], ["cjb"])
+        ts(T.mod[:], T.cj[:, 0:128], 0.0, Op.is_equal, ["cja"], ["mod"])
+        ts(T.m8[:], T.cj[:, 128:136], 0.0, Op.is_equal, ["cjb"], ["m8"])
+        ts(T.tril[:], T.ci[:, 0:128], 128.0, Op.is_gt, ["cia"], ["tril"])
+        for t in range(3):
+            ts(T.ca[:, 512 * t + t:512 * t + 512:4], T.mod[:], 0.0, Op.mult, ["mod", "ca"], ["ca.%d" % t], 32.0 ** t, Op.add)
+            ts(T.cb[:, 512 * t + t:512 * t + 512:4], T.mod[:], 32.0 ** t, Op.mult, ["mod", "cb"], ["cb.%d" % t])
+        quant(T.qa[:], T.sa[:], T.ca[:], ["ca"] + ["ca.%d" % t for t in range(3)], ["qa"])
+        quant(T.qb[:], T.sb[:], T.cb[:], ["cb"] + ["cb.%d" % t for t in range(3)], ["qb"])
+        quant(T.qu[:], T.su[:], T.ui[:], ["ui"], ["qu"])
+        ts(sm("jw"), T.nat[:, 0:8], 16.0, Op.mult, ["nat", "pf"], ["jw"], pf(0), Op.add)
+        ts(pf(19), pf(7), 16.0, Op.mult, ["pf"], ["pf19"])
+        ts(pf(20), pf(8), -128.0, Op.mult, ["pf"], ["pf20"], 129.0, Op.add)
+        ts(sm("jd"), sm("jw"), 320.0, Op.add, ["jw"], ["jd"])
+        ts(T.nat512[:], T.nat[:], 512.0, Op.mult, ["nat"], ["nat512"])
+        ts(T.yy[:, 32:33], pf(9), 1024.0, Op.mult, ["pf"], ["yyc"])
+        ts(T.la[:, 0:2], T.cf[:, 56:58], pf(19), Op.add, ["cf3", "pf19"], ["la0"])
+        tt(pf(21), pf(20), pf(19), Op.add, ["pf20", "pf19"], ["pf21"])
+        ts(T.la[:, 2:4], T.nat[:, 0:2], 0.0, Op.mult, ["nat", "pf21"], ["la1"], pf(21), Op.add)
+
+    def candidates_a():
+        cp(T.rle[:], T.ox[:, 0:512].indirect(T.lr[:]), ["ox%d" % k for k in range(8)] + ["lr"], ["rle"])
+        tr(T.te[:], T.rle[:], ["rle"], ["te"])
+        cp(T.ew[:], T.te[:].indirect(T.pk[:, 2:3]), ["te", "pk1"], ["ew"])
+        ts(T.e1[:], T.ew[:, 0:8], 15, Op.bitwise_and, ["ew"], ["e1"])
+        ts(T.e2[:], T.ew[:, 0:8], 4, Op.logical_shift_right, ["ew"], ["e2"])
+        cp(T.el[:], T.ew[:, 0:8], ["ew"], ["el"])
+        ts(T.ec[:], T.e1[:], 80.0, Op.mult, ["e1"], ["ec"])
+        tt(T.e1[:], T.ec[:], T.e2[:], Op.add, ["ec", "e2"], ["e1"])
+        for k in range(4):
+            ts(T.lc[:, 8 * k:8 * k + 8], T.e1[:], 20.0 * k, Op.add, ["e1"], ["lc%d" % k])
+
+    def candidates_b():
+        act(T.rf[:, 4:768:6], T.nat[:].indirect(T.lw[:, 0:8]), ["nat", "lw"], ["rf4"])
+        act(T.rf[:, 5:768:6], T.nat[:].indirect(T.el[:]), ["nat", "el", "pf22"], ["rf5"], func=Act.Identity, scale=1024.0, bias=pf(22))
+        for k in range(4):
+            act(T.rf[:, k:768:6], T.cwf[:].indirect(T.lc[:, 8 * k:8 * k + 8]), ["cwf", "lc%d" % k], ["rf%d" % k])
+        for gr in range(8):
+            dma("y", "dc", T.cp[:, 6 * gr:6 * gr + 6], T.rf[16 * gr:16 * gr + 1, 0:768], ["rf%d" % k for k in range(6)], ["cp%d" % gr])
+
+    def candidates_c():
+        C = ["cp%d" % k for k in range(8)]
+        for k in range(4):
+            tt(T.ne[:, 8 * k:8 * k + 8], T.cp[:, k:48:6], T.cp[:, 4:48:6], Op.not_equal, C, ["ne%d" % k])
+            tt(T.sk[:, 8 * k:8 * k + 8], T.cp[:, k:48:6], T.cp[:, 5:48:6], Op.add, C, ["sk%d" % k])
+        tt(T.pp[:], T.ne[:], T.sk[:], Op.mult, ["ne%d" % k for k in range(4)] + ["sk%d" % k for k in range(4)], ["pp"])
+
+    def make_h(k, wc, wp, wkeys, mc, mp, mkey, engines):
+        for b in range(4):
+            c = slice(128 * b, 128 * b + 128)
+            mm(PS[b][:, 0:128], wc[:, c], wp[:, c], mc[:], mp[:], wkeys + [mkey], ["#%d" % b])
+        for b in range(4):
+            if engines[b] == "s":
+                act(T.ht[:, b:512:4], PS[b][:, 0:128], ["#%d" % b], [H4[b]], func=Act.Relu, scale=0.03125)
+            else:
+                ts(T.ht[:, b:512:4], PS[b][:, 0:128], 0.0, Op.max, ["#%d" % b], [H4[b]], 0.03125, Op.mult)
+        quant(T["qh%d" % k][:], T["sh%d" % k][:], T.ht[:], H4, ["qh%d" % k])
+
+    def state_lists():
+        tt(sm("wn"), sm("fi"), sm("jw"), Op.is_equal, ["fi%d" % c for c in range(8)] + ["jw"], ["wn"])
+        ts(sm("xd"), sm("nl"), -1.0 / 512, Op.mult, ["nl"], ["xd"])
+        tt(sm("xd"), sm("xd"), sm("jd"), Op.subtract, ["xd", "jd"], ["xd"])
+        tt(sm("xd"), sm("xd"), sm("wn"), Op.mult, ["xd", "wn"], ["xd"])
+        tt(sm("xd"), sm("xd"), sm("jd"), Op.add, ["xd", "jd"], ["xd"])
+        for t in range(4):
+            ts(T.xl[:, 8 * t:8 * t + 8], sm("xd"), 4.0, Op.mult, ["xd"], ["xl%d" % t], float(t), Op.add)
+
+    def scatter_state():
+        for t in range(4):
+            cp(T.xt[:].indirect(T.xl[:, 8 * t:8 * t + 8]), T.nt[:, t:512:4], ["xl%d" % t, N4[t]], X4)
+        quant(T.qx[:], T.sx[:], T.xt[:, 0:1280], X4, ["qx"])
+
+    for k in range(3):
+        donor, client = T.cores[(r + STEP[k]) % N], T.cores[(r - STEP[k]) % N]
+        qm, sm_, qh, sh = T["qm%d" % k], T["sm%d" % k], T["qh%d" % k], T["sh%d" % k]
+        if k == 0:
+            for t in range(4):
+                src = T.fh[:, 320 * t:320 * t + 320].indirect(T.lw[:, 0:8])
+                if t % 2 == 0:
+                    act(T.mt[:, t:512:4], src, ["fh%d" % t, "lw"], [M4[t]], scale=2.0)
+                else:
+                    ts(T.mt[:, t:512:4], src, 2.0, Op.mult, ["fh%d" % t, "lw"], [M4[t]])
+        else:
+            quant(T.qn[:], T.sn[:], T.nt[:], N4, ["qn"])
+            for t in range(4):
+                mm(PS[t][:, 0:128], T.qe[:, 128 * t:128 * t + 128], T.se[:, 128 * t:128 * t + 128], T.qn[:], T.sn[:], ["qe", "qn"], ["#%d" % t])
+            if k == 2:
+                candidates_a()
+            for t in range(4):
+                if t % 2 == 0:
+                    act(T.mt[:, t:512:4], PS[t][:, 0:128], ["#%d" % t], [M4[t]])
+                else:
+                    cp(T.mt[:, t:512:4], PS[t][:, 0:128], ["#%d" % t], [M4[t]])
+        quant(qm[:], sm_[:], T.mt[:], M4, ["qm%d" % k])
+        if k == 0:
+            dst = T.cores[(r - STEP[2]) % N]
+            send([(T.wdc[:].bitcast(B8), T.wcs[:].bitcast(B8)), (T.wdp[:], T.wps[:])], dst, "aw", ["wcs", "wps"])
+            arrives("aw", T.cores[(r + STEP[2]) % N], ["wd"])
+        if k < 2:
+            send([(T["mc%d" % k][:].bitcast(B8), qm[:].bitcast(B8)), (T["mp_%d" % k][:], sm_[:])], donor, "am%d" % k, ["qm%d" % k])
+            arrives("am%d" % k, client, ["mc%d" % k])
+            if k == 0:
+                cp(T.cwf[:], T.cwi[:], ["cwi%d" % i for i in range(16)], ["cwf"])
+                ts(pf(22), pf(3), -327680.0, Op.mult, ["pf"], ["pf22"], 2621440.0, Op.add)
+            candidates_a()
+            candidates_b()
+            make_h(k, T.wcs, T.wps, ["wcs", "wps"], T["mc%d" % k], T["mp_%d" % k], "mc%d" % k, "svsv")
+            send([(T["hc%d" % k][:].bitcast(B8), qh[:].bitcast(B8)), (T["hp%d" % k][:], sh[:])], client, "ah%d" % k, ["qh%d" % k])
+            arrives("ah%d" % k, donor, ["hc%d" % k])
+            hc, hp, hkey = T["hc%d" % k], T["hp%d" % k], "hc%d" % k
+        else:
+            candidates_b()
+            make_h(k, T.wdc, T.wdp, ["wd"], qm, sm_, "qm2", "vvvv")
+            hc, hp, hkey = qh, sh, "qh2"
+        if k:
+            scatter_state()
+            decode_x()
+        else:
+            more_constants()
+        candidates_c()
+        mm(PS[4][:, 0:128], hc[:], hp[:], T.qu[:], T.su[:], [hkey, "qu"], ["#4"])
+        for t in range(4):
+            mm(PS[t][:, 0:128], T.qe[:, 128 * t:128 * t + 128], T.se[:, 128 * t:128 * t + 128], hc[:], hp[:], ["qe", hkey], ["#%d" % t])
+        ts(T.sg[:, 0:128], PS[4][:, 0:128], 0.0, Op.is_gt, ["#4"], ["sg0"])
+        ts(T.sg[:, 128:256], PS[4][:, 0:128], 0.0, Op.is_le, ["#4"], ["sg1"])
+        tt(T.xx[:], T.sg[:].indirect(T.la[:, 0:2]), T.pp[:], Op.mult, ["sg0", "sg1", "la0", "pp"], ["xx"])
+        tt(T.yy[:, 0:32], T.sg[:].indirect(T.la[:, 2:4]), T.xx[:], Op.mult, ["sg0", "sg1", "la1", "xx"], ["yy"])
+        red(sm("rq", 1), T.yy[:, 0:33], Op.max, ["yy", "yyc"], ["rq"])
+        ts(T.qd[:, 0:6], sm("sc", 6), sm("rq", 1), Op.mult, ["rq"] + ["sc%d" % t for t in range(6)], ["qd"])
+        ts(sm("nq", 5), T.qd[:, 1:6], -32.0, Op.mult, ["qd"], ["nq"])
+        tt(sm("dg", 5), sm("nq", 5), T.qd[:, 0:5], Op.add, ["nq", "qd"], ["dg"])
+        dg = lambda t: T.fs[:, SMALL["dg"] + t:SMALL["dg"] + t + 1]
+        for t in range(3):
+            ts(T.b1[:, t:512:4], T.idb[:], dg(2 + t), Op.mult, ["idb", "dg", "b1"], ["ba%d" % t])
+        quant(T.qk[:, 0:128], T.sk1[:, 0:128], T.b1[:, 0:512], ["ba%d" % t for t in range(3)] + ["b1"], ["qk0"])
+        for t in range(3):
+            mm(PS[5][:, 0:128], T.qa[:, 128 * t:128 * t + 128], T.sa[:, 128 * t:128 * t + 128], T.qk[:, 0:128], T.sk1[:, 0:128], ["qa", "qk0"], ["#5"], t == 0, t == 2)
+        for t in range(2):
+            act(T.b1[:, 512 + t:1024:4], T.idb[:], ["idb", "dg", "b1"], ["bb%d" % t], scale=dg(t))
+        for t in range(3):
+            ts(T.b1[:, 1024 + t:1056:4], T.m8[:], dg(2 + t), Op.mult, ["m8", "dg", "b1"], ["bc%d" % t])
+        ts(sm("kf", 1), T.qd[:, 2:3], 1.0, Op.add, ["qd"], ["kf"])
+        quant(T.qk[:, 256:384], T.sk1[:, 256:384], T.b1[:, 1024:1536], ["bc0", "bc1", "bc2", "b1"], ["qk2"])
+        for t in range(3):
+            mm(PS[7][:, 0:128], T.qb[:, 128 * t:128 * t + 128], T.sb[:, 128 * t:128 * t + 128], T.qk[:, 256:384], T.sk1[:, 256:384], ["qb", "qk2"], ["#7"], t == 0, t == 2)
+        act(sm("kw"), PS[7][:, 0:8], ["#7"], ["kw"])
+        ts(T.kt[:], T.tril[:], sm("kf", 1), Op.mult, ["tril", "kf"], ["kt"], -1.0, Op.add)
+        tt(T.eq[:], PS[5][:, 0:128], T.kt[:], Op.is_equal, ["#5", "kt"], ["eq"])
+        red(sm("lo", 1), T.eq[:], Op.max, ["eq"], ["lo"])
+        ts(T.b2[:, 0:32:4], T.m8[:], sm("lo", 1), Op.mult, ["m8", "lo", "b2"], ["b2a"])
+        quant(T.ql[:], T.sl[:], T.b2[:], ["b2", "b2a"], ["ql"])
+        mm(PS[4][:, 0:128], T.qb[:, 0:128], T.sb[:, 0:128], T.ql[:], T.sl[:], ["qb", "ql"], ["#4"])
+        quant(T.qk[:, 128:256], T.sk1[:, 128:256], T.b1[:, 512:1024], ["bb0", "bb1", "b1"], ["qk1"])
+        for t in range(2):
+            mm(PS[6][:, 0:128], T.qa[:, 128 * t:128 * t + 128], T.sa[:, 128 * t:128 * t + 128], T.qk[:, 128:256], T.sk1[:, 128:256], ["qa", "qk1"], ["#6"], t == 0, t == 1)
+        act(T.va[:], PS[6][:, 0:128], ["#6"], ["va"])
+        for t in range(4):
+            act(T.dh[:, 128 * t:128 * t + 128], PS[t][:, 0:128], ["#%d" % t], ["dh%d" % t], scale=0.5)
+        base_x()
+        tt(sm("dj"), sm("jw"), sm("kw"), Op.subtract, ["jw", "kw"], ["dj"])
+        tt(sm("t1"), PS[4][:, 0:8], sm("dj"), Op.mult, ["#4", "dj"], ["t1"])
+        tt(sm("t2"), sm("t1"), sm("kw"), Op.add, ["t1", "kw"], ["t2"])
+        cp(T.ofs[:], sm("t2"), ["t2"], ["ofs"])
+        cp(T.fw[:].indirect(T.ofs[:]), T.va[:], ["ofs", "va"], FWALL + ["fwd"])
+        if k == 2:
+            for gr in range(8):
+                dma("y", "do", T.fo[gr:gr + 1, :], T.fw[0:1, 320 * (8 - gr):320 * (8 - gr) + 320], ["fw%d" % gr], [])
+        for s in range(8):
+            step_a(s)
+            if s < 7:
+                step_b(s)
+                step_c(s)
+        places()
+        ts(sm("nl"), T.lw[:, 0:8], -512.0, Op.mult, ["lw"], ["nl"])
+        tt(T.kk[:], T.nat512[:].indirect(T.lw[:, 0:8]), T.nat[:, 0:128], Op.add, ["nat512", "lw", "nat"], ["kk"])
+        for c in range(8):
+            d, b = T.dd[:, 128 * c:128 * c + 128], T.fs[:, SMALL["nl"] + c:SMALL["nl"] + c + 1]
+            if c in (0, 3, 6):
+                ts(d, T.kk[:], b, Op.add, ["kk", "nl"], ["dd%d" % c])
+            else:
+                act(d, T.kk[:], ["kk", "nl"], ["dd%d" % c], func=Act.Identity, bias=b)
+        for c in (0, 1, 3, 2, 6, 4, 5, 7):
+            red(T.fs[:, SMALL["fi"] + c:SMALL["fi"] + c + 1], T.dd[:, 128 * c:128 * c + 128], Op.min, ["dd%d" % c], ["fi%d" % c], apply_absolute_value=True)
+        for t in range(4):
+            act(T.fg[:, 128 * t:128 * t + 128], T.fh[:, 320 * t:320 * t + 320].indirect(T.lw[:, 0:8]), ["fh%d" % t, "lw"], ["fg%d" % t])
+        cp(T.fl[:], sm("fi"), ["fi%d" % c for c in range(8)], ["fl"])
+        if k == 2:
+            state_lists()
+        for t in range(4):
+            tt(T.nt[:, t:512:4], T.dh[:, 128 * t:128 * t + 128].indirect(T.fl[:]), T.fg[:, 128 * t:128 * t + 128], Op.add, ["dh%d" % t, "fl", "fg%d" % t], [N4[t]])
+        if k < 2:
+            state_lists()
+    quant(T.qv[:], T.sv[:], T.vi[:], ["vi"], ["qv"])
+    scatter_state()
+    mm(PS[4][:, 0:320], T.qv[:], T.sv[:], T.qx[:], T.sx[:], ["qv", "qx"], ["#4"])
+    dma("y", "do", T.oc[:], T.qx[:].bitcast(B8), ["qx"], [])
+    for i in range(4):
+        dma("s" if i % 2 else "y", "do", T.osc[4 * i:4 * i + 4, :], T.sx[32 * i:32 * i + 4, :], ["qx"], [])
+    cp(T.yo[:], PS[4][:, 0:320], ["#4"], ["yo"])
+    dma("s", "do", T.y[:], T.yo[:], ["yo"], [])
+    for sem in sorted(tot):
+        if known["p"].get(sem, 0) < tot[sem]:
+            g.wait_ge(T.sem[sem], tot[sem])

@@ -1,175 +1,137 @@
 from concourse.mybir import dt, AluOpType as Op, AxisListType, ActivationFunctionType as Act
 
 F32, BF, I32, U16, MXC, U8 = "float32", "bfloat16", "int32", "uint16", "float8_e4m3fn_x4", "uint8"
-SCRATCH = {
-    "xi": ("sbuf", [128, 1280], BF), "ui": ("sbuf", [128, 512], BF), "vi": ("sbuf", [128, 512], BF),
-    "mwi": ("sbuf", [128, 192], I32), "mwf": ("sbuf", [128, 192], F32),
-    "cwi": ("sbuf", [128, 1280], I32), "cwf": ("sbuf", [128, 1280], F32),
-    "wcs": ("sbuf", [128, 512], MXC), "wps": ("sbuf", [128, 512], U8),
-    "wdc": ("sbuf", [128, 512], MXC), "wdp": ("sbuf", [128, 512], U8),
-    "pi": ("sbuf", [128, 16], I32), "pf": ("sbuf", [128, 32], F32), "nat": ("sbuf", [128, 320], F32), "nat512": ("sbuf", [128, 320], F32),
-    "ci": ("sbuf", [128, 160], I32), "cj": ("sbuf", [128, 160], I32), "cf": ("sbuf", [128, 192], F32),
-    "tril": ("sbuf", [128, 128], F32), "idb": ("sbuf", [128, 128], BF), "mod": ("sbuf", [128, 128], BF), "m8": ("sbuf", [128, 8], BF),
-    "l0": ("sbuf", [128, 4], U16), "lr": ("sbuf", [128, 8], U16), "ly": ("sbuf", [128, 20], U16), "pk": ("sbuf", [128, 4], U16),
-    "la": ("sbuf", [128, 4], U16),
-    "zt": ("sbuf", [128, 512], BF), "ce": ("sbuf", [128, 2048], BF), "ca": ("sbuf", [128, 1536], BF), "cb": ("sbuf", [128, 1536], BF),
-    "qe": ("sbuf", [128, 512], MXC), "se": ("sbuf", [128, 512], U8),
-    "qa": ("sbuf", [128, 384], MXC), "sa": ("sbuf", [128, 384], U8),
-    "qb": ("sbuf", [128, 384], MXC), "sb": ("sbuf", [128, 384], U8),
-    "qu": ("sbuf", [128, 128], MXC), "su": ("sbuf", [128, 128], U8),
-    "qv": ("sbuf", [128, 128], MXC), "sv": ("sbuf", [128, 128], U8),
-    "fs": ("sbuf", [128, 192], F32),
-    "yb": ("sbuf", [128, 2560], F32), "fw": ("sbuf", [128, 2880], F32),
-    "ox": ("sbuf", [128, 576], F32), "tt": ("sbuf", [128, 448], F32), "of": ("sbuf", [128, 32], U16),
-    "rl": ("sbuf", [128, 128], F32), "tl": ("sbuf", [128, 128], F32), "lw": ("sbuf", [128, 16], U16),
-    "rle": ("sbuf", [128, 128], F32), "te": ("sbuf", [128, 128], F32), "ew": ("sbuf", [128, 16], I32),
-    "e1": ("sbuf", [128, 8], I32), "e2": ("sbuf", [128, 8], I32), "ec": ("sbuf", [128, 8], I32), "el": ("sbuf", [128, 8], U16), "lc": ("sbuf", [128, 32], U16),
-    "rf": ("sbuf", [128, 768], F32), "cp": ("sbuf", [128, 48], F32),
-    "ne": ("sbuf", [128, 32], F32), "sk": ("sbuf", [128, 32], F32), "pp": ("sbuf", [128, 32], F32),
-    "kk": ("sbuf", [128, 128], F32), "dd": ("sbuf", [128, 1024], F32), "fl": ("sbuf", [128, 8], U16),
-    "sg": ("sbuf", [128, 256], F32), "xx": ("sbuf", [128, 32], F32), "yy": ("sbuf", [128, 36], F32),
-    "qd": ("sbuf", [128, 8], I32),
-    "b1": ("sbuf", [128, 1536], BF), "b2": ("sbuf", [128, 512], BF),
-    "qk": ("sbuf", [128, 384], MXC), "sk1": ("sbuf", [128, 384], U8), "ql": ("sbuf", [128, 128], MXC), "sl": ("sbuf", [128, 128], U8),
-    "kt": ("sbuf", [128, 128], F32), "eq": ("sbuf", [128, 128], F32), "ofs": ("sbuf", [128, 8], U16),
-    "va": ("sbuf", [128, 128], F32),
-    "fh": ("sbuf", [128, 1280], BF), "dh": ("sbuf", [128, 512], BF), "fg": ("sbuf", [128, 512], F32),
-    "nt": ("sbuf", [128, 512], BF), "qn": ("sbuf", [128, 128], MXC), "sn": ("sbuf", [128, 128], U8),
-    "mt": ("sbuf", [128, 512], BF), "ht": ("sbuf", [128, 512], BF),
-    "xt": ("sbuf", [128, 1792], BF), "qx": ("sbuf", [128, 320], MXC), "sx": ("sbuf", [128, 320], U8),
-    "xl": ("sbuf", [128, 32], U16), "yo": ("sbuf", [128, 320], F32),
-}
-for _r in range(3):
-    SCRATCH["qm%d" % _r] = ("sbuf", [128, 128], MXC)
-    SCRATCH["sm%d" % _r] = ("sbuf", [128, 128], U8)
-    SCRATCH["qh%d" % _r] = ("sbuf", [128, 128], MXC)
-    SCRATCH["sh%d" % _r] = ("sbuf", [128, 128], U8)
-    if _r < 2:
-        SCRATCH["mc%d" % _r] = ("sbuf", [128, 128], MXC)
-        SCRATCH["mp_%d" % _r] = ("sbuf", [128, 128], U8)
-        SCRATCH["hc%d" % _r] = ("sbuf", [128, 128], MXC)
-        SCRATCH["hp%d" % _r] = ("sbuf", [128, 128], U8)
-for _r in range(8):
-    SCRATCH["p%d" % _r] = ("psum", [128, 512], F32)
-SMALL = {n: 8 * k for k, n in enumerate(("jw", "jd", "sc", "nq", "dg", "kf", "lo", "kw", "dj", "t1", "t2", "rq", "fi", "wn", "xd", "nl"))}
-SEMAPHORES = ["v", "s", "t", "p", "dx", "du", "dv", "dw", "da", "dc", "do", "aw", "am0", "am1", "ah0", "ah1", "ls"] + ["dm%d" % _r for _r in range(8)]
+SCRATCH = {}
+for _n, _w, _t in (
+        ("xi", 1280, BF), ("ui", 512, BF), ("vi", 512, BF), ("mwi", 192, I32), ("mwf", 192, F32), ("cwi", 1280, I32), ("cwf", 1280, F32),
+        ("wcs", 512, MXC), ("wps", 512, U8), ("wdc", 512, MXC), ("wdp", 512, U8),
+        ("pi", 16, I32), ("pf", 32, F32), ("nat", 320, F32), ("nat512", 320, F32), ("ci", 160, I32), ("cj", 160, I32), ("cf", 192, F32), ("k20", 32, I32),
+        ("tril", 128, BF), ("idb", 128, BF), ("mod", 128, BF), ("m8", 8, BF),
+        ("l0", 4, U16), ("lr", 8, U16), ("lr7", 8, U16), ("ly", 20, U16), ("pk", 4, U16), ("la", 4, U16),
+        ("zt", 512, BF), ("ce", 2048, BF), ("ca", 1536, BF), ("cb", 1536, BF),
+        ("qe", 512, MXC), ("se", 512, U8), ("qa", 384, MXC), ("sa", 384, U8), ("qb", 384, MXC), ("sb", 384, U8),
+        ("qu", 128, MXC), ("su", 128, U8), ("qv", 128, MXC), ("sv", 128, U8), ("fs", 192, F32),
+        ("yb", 2560, F32), ("fw", 2880, F32), ("ox", 512, F32), ("o7", 128, F32), ("tt", 448, F32), ("of", 40, U16),
+        ("rl", 128, F32), ("tl", 256, F32), ("lw", 16, U16), ("rle", 128, F32), ("te", 128, F32), ("ew", 32, I32),
+        ("e1", 32, I32), ("e2", 32, I32), ("e3", 32, I32), ("ec", 32, I32), ("el", 8, U16), ("lc", 32, U16),
+        ("rf", 768, F32), ("cp", 48, F32), ("ne", 32, F32), ("sk", 32, F32), ("pp", 32, F32), ("kk", 128, F32), ("dd", 1024, F32), ("fl", 8, U16),
+        ("sg", 32, F32), ("xx", 32, F32), ("yy", 36, F32), ("qd", 8, I32), ("b1", 1536, BF), ("b2", 512, BF),
+        ("qk", 384, MXC), ("sk1", 384, U8), ("ql", 128, MXC), ("sl", 128, U8), ("kt", 128, F32), ("eq", 128, F32), ("ofs", 8, U16), ("va", 128, F32),
+        ("fh", 1280, BF), ("dh", 512, BF), ("fg", 512, F32), ("nt", 512, BF), ("qn", 128, MXC), ("sn", 128, U8), ("mt", 512, BF), ("ht", 512, BF),
+        ("xt", 1792, BF), ("qx", 320, MXC), ("sx", 320, U8), ("xl", 32, U16), ("yo", 320, F32),
+        ("qm0", 128, MXC), ("sm0", 128, U8), ("qm1", 128, MXC), ("sm1", 128, U8), ("qm2", 128, MXC), ("sm2", 128, U8),
+        ("qh0", 128, MXC), ("sh0", 128, U8), ("qh1", 128, MXC), ("sh1", 128, U8), ("qh2", 128, MXC), ("sh2", 128, U8),
+        ("mc0", 128, MXC), ("mp_0", 128, U8), ("mc1", 128, MXC), ("mp_1", 128, U8), ("hc0", 128, MXC), ("hp0", 128, U8), ("hc1", 128, MXC), ("hp1", 128, U8)):
+    SCRATCH[_n] = ("sbuf", [128, _w], _t)
+for _n in range(8):
+    SCRATCH["p%d" % _n] = ("psum", [128, 512], F32)
+SMALL = {n: 8 * k for k, n in enumerate(("jw", "jd", "sc", "nq", "dg", "kf", "lo", "kw", "dj", "t1", "t2", "rq", "fi", "wn", "xd", "nl", "xe"))}
+SEMAPHORES = ["v", "s", "t", "p", "dx", "du", "dv", "dw", "da", "dc", "do", "aw", "am0", "am1", "ah0", "ah1", "ls"] + ["dm%d" % _n for _n in range(8)]
 STEP = [1, 2, 3]
+ORDER_TEXT = """
+1 61 93 120 24 49 94 15 0 52 2 110 112 3-4 97 113 5-6 115 7 41 116 22 8 117-118 30 10 111 11-12 114 13-14 46 63 119 9 17-19 121 20-21 122 98 126
+23 26 35 28 141 123 25 32 124 27 34 130 29 36 128 31 38 125 131 37 42 134 39 44 127 16 48 234 33 50 135 47 54 136 57 56 51 60 53 62 55 58 95 59
+40 43 64 99 45 145 132 75 139 66 146 133 73 137 67 129 68-69 151 140 71-72 152 74 157 76 78-81 163 100 147 82 158 77 65 90 153 70 91 83-84 148
+164 85-87 149 88 159 89 92 101 150 169 154 170 155 165 156 175 160 176 102 161 171 162 181 166 182 167 177 168 96 187 172 188 183 106 105 173
+103 193 108 192 104 189 194 109 174 195 138 198 178 107 196 179-180 199 197 184-185 200 256 186 202 190 201 235 203 191 257 291 204 258 237 236*
+238* 239 268 240 259 293 241 233 294 242-243 292 260-265 269 266-267 142 272 270 273 227 223 271 211 205-206 208 279 209 274 210 275 213 277 144
+278 280-281 276 247 244 251* 245-246 248 249* 229 250 226 252 231 230 253 216 220 212 143 254-255 283 282 284-286 289 217 219 288 214 287 207
+225 215 290 221 232 218 228 222 224 295 340 296 337 297 344 338 298 339 341 299-300 343 301 342 302 316 303 322 315 313* 304-305* 311 306* 314*
+307 312 317 308-309 328 310 318 323 319-320 324 329 321* 330 325 332 326 331 327 333-336 345-364 368 365 369 366-367 370-371 392 372 389 390* 391
+379-380 377 442 373-374 381 378* 382 376 388 375* 387 384 383 386 385 393 403 405-406 404 407 432 411 409 395 415* 410 413* 408 414* 412* 416 433
+417 394 434 396 435-436 418 437 439 443 438 397 440 419 398 441 400 399 444 447* 445 446* 465 454 452 448 450 449 451 401 455 466 453 402 467-469
+421 420 425* 422 424 423 426 471 427 462 428 472 475 463 456 429 457 473 458-461 476 470 430 464 477* 479 431 474* 480-481* 478* 482 525 483 524
+484 529 526 485 527 530 486-487 528 488 531 489 503 490 509 502 493* 491-492* 498 501* 494 499-500* 495-496 504 497 515 505 510 506-507 511 516
+508* 517 512 519 513 518 514 520-523 532-551 555 552 613 553-554 614 556 615 557 617 616 623 619 559 577 620 558 578 618 621 564 567 624 566 565
+579 560-562 575-576 574 573 563* 572 568-571 622 580 625* 626 627* 628 590 629-630 591 632-634 592 635-636 631 593 582 594 583 581 598 597 584
+602* 595 601* 596 599-600* 585 603 586-587 605 646 604 609* 606-607 610* 608 637 611* 638-642 612 643-644 663 645 664-670 684 671 690 682 672*
+680* 673* 679 683* 681* 674* 685 675 686 696 687 647 676-678 688 691 697 689* 698 692 700 699 693 588 694 589 648 695 701-704 721 718 713-715 722
+716 723 717 719 724 720 725-727 649 728-734 650 735 651 736 652 737 655 738 653 739 656 654 740 744 705 741 658 742 706 745 657 743 708 746 712*
+765 748 707 747 766 711* 753 756 767 755 754 768 763 762 749 752* 751 764 750* 761 771 709 757 759-760 758 710 772 660* 662 770 769 661* 773 659
+774 779 775 780 783 776 781 784 777-778 785 782 786-789 791-793 790 794* 795
+"""
 
 
-def rank_program(g, core, T, topo):
+def program(g, core, T, topo):
     r = T.rank_of(core)
-    if r is None:
-        return
     N = len(T.cores)
     Q = {"v": g.vector, "s": g.scalar, "t": g.tensor, "p": g, "y": g.sync}
-    known = {q: {} for q in Q}
-    tot, wr, rd = {}, {}, {}
-
-    def gate(q, reads, writes, acc=False):
-        toks = []
-        for k in reads:
-            toks += wr.get(k, [])
-            if k[0] == "#":
-                toks += [t for t in rd.get(k, []) if t[3] != q]
-        for k in writes:
-            if not acc:
-                toks += wr.get(k, [])
-            toks += rd.get(k, [])
-        want = {}
-        for sem, val, snap, _ in toks:
-            if isinstance(val, tuple):
-                val = val[0] if known[q].get(sem, 0) >= val[0] else tot[sem]
-            if val > want.get(sem, (0, None))[0]:
-                want[sem] = (val, snap)
-        for sem in sorted(want, key=lambda m: -len(want[m][1])):
-            val, snap = want[sem]
-            if known[q].get(sem, 0) < val:
-                Q[q].wait_ge(T.sem[sem], val)
-                known[q][sem] = val
-                for a, b in snap.items():
-                    known[q][a] = max(known[q].get(a, 0), b)
-
-    def note(tok, reads, writes):
-        for k in reads:
-            rd.setdefault(k, []).append(tok)
-        for k in writes:
-            wr[k] = [tok]
-            rd[k] = []
+    ops = []
 
     def op(q, call, reads, writes, acc=False):
-        gate(q, reads, writes, acc)
-        tot[q] = tot.get(q, 0) + 1
-        call().then_inc(T.sem[q], 1)
-        note((q, tot[q], dict(known[q]), q), reads, writes)
+        ops.append([q, call, reads, writes, "acc" if acc else "op", None, 0])
 
-    def dma(q, sem, out, in_, reads, writes):
-        gate(q, reads, writes)
-        tot[sem] = tot.get(sem, 0) + 16
-        Q[q].dma_start(out, in_).then_inc(T.sem[sem], 16)
-        note((sem, (tot[sem],), dict(known[q]), sem), reads, writes)
+    def dma(q, sem, out, in_, reads, writes, batch=0):
+        ops.append([q, lambda _: Q[q].dma_start(out, in_), reads, writes, "dma", sem, batch])
 
     def send(pairs, dst, sem, reads):
-        gate("p", reads, [])
         rid, pid, _ = topo.addr(dst)
-        mask = topo.mask(core, dst)
+        mask, n = topo.mask(core, dst), len(topo.engines(core, dst))
         for out, in_ in pairs:
-            g.remote_dma(out, in_, T.sem[sem], T.sem.ls, pid, rid, mask)
-            tot["ls"] = tot.get("ls", 0) + len(topo.engines(core, dst))
+            ops.append(["p", lambda _, out=out, in_=in_: g.remote_dma(out, in_, T.sem[sem], T.sem.ls, pid, rid, mask), reads, ["sent." + sem], "send", sem, n])
 
     def arrives(sem, src, writes):
-        tot[sem] = 2 * len(topo.engines(src, core))
-        for k in writes:
-            wr[k] = [(sem, tot[sem], {}, sem)]
+        ops.append(["-", None, ["sent." + sem], writes, "arrival", sem, 2 * len(topo.engines(src, core))])
 
     V, S = g.vector, g.scalar
     B8 = dt.uint8
 
-    def ts(q_out, in0, s1, op0, reads, writes, s2=None, op1=None):
+    def ts(out, in0, s1, op0, reads, writes, s2=None, op1=None):
         if op1 is None:
-            op("v", lambda: V.tensor_scalar(q_out, in0, s1, None, op0), reads, writes)
+            op("v", lambda _: V.tensor_scalar(out, in0, s1, None, op0), reads, writes)
         else:
-            op("v", lambda: V.tensor_scalar(q_out, in0, s1, s2, op0, op1), reads, writes)
+            op("v", lambda _: V.tensor_scalar(out, in0, s1, s2, op0, op1), reads, writes)
 
     def tt(out, a, b, o, reads, writes):
-        op("v", lambda: V.tensor_tensor(out, a, b, o), reads, writes)
+        op("v", lambda _: V.tensor_tensor(out, a, b, o), reads, writes)
 
     def cp(out, in_, reads, writes):
-        op("v", lambda: V.tensor_copy(out, in_), reads, writes)
+        op("v", lambda _: V.tensor_copy(out, in_), reads, writes)
 
     def tr(out, in_, reads, writes):
-        op("v", lambda: V.transpose(out, in_), reads, writes)
+        op("v", lambda _: V.transpose(out, in_), reads, writes)
 
-    def act(out, in_, reads, writes, func=Act.Copy, **kw):
-        op("s", lambda: S.activation(out, in_, func, **kw), reads, writes)
+    def times(out, in_, reads, writes, scale, q="sv"):
+        op(q, lambda e: S.activation(out, in_, Act.Copy, scale=scale) if e == "s" else V.tensor_scalar(out, in_, scale, None, Op.mult), reads, writes)
 
     def red(out, in_, o, reads, writes, **kw):
-        op("v", lambda: V.tensor_reduce(out, in_, AxisListType.X, o, **kw), reads, writes)
+        op("v", lambda _: V.tensor_reduce(out, in_, AxisListType.X, o, **kw), reads, writes)
 
     def fill(ap, val, writes):
-        op("v", lambda: V.memset(ap, val), [], writes)
+        op("v", lambda _: V.memset(ap, val), [], writes)
 
     def quant(q, s, t, reads, writes):
-        op("v", lambda: V.quantize_mx(q, s, t), reads, writes)
+        op("v", lambda _: V.quantize_mx(q, s, t), reads, writes)
 
     def mm(out, l, ls, m, ms, reads, writes, start=True, stop=True):
-        op("t", lambda: g.tensor.matmul_mx(out, l, ls, m, ms, start, stop), reads, writes, acc=not start)
+        op("t", lambda _: g.tensor.matmul_mx(out, l, ls, m, ms, start, stop), reads, writes, acc=not start)
 
     def iota(out, pattern, base, cm, writes, flt):
         if flt:
-            op("p", lambda: g.iota(out, pattern, base, cm, allow_small_or_imprecise_dtypes=True), [], writes)
+            op("p", lambda _: g.iota(out, pattern, base, cm, allow_small_or_imprecise_dtypes=True), [], writes)
         else:
-            op("p", lambda: g.iota(out, pattern, base, cm), [], writes)
+            op("p", lambda _: g.iota(out, pattern, base, cm), [], writes)
+
+    def select(out, in_, pattern, cmp, fill_, base, cm, reads, writes):
+        op("p", lambda _: g.affine_select(out, in_, pattern, cmp, fill_, base, cm), reads, writes)
+
+    def col(name, k, n=1):
+        return T[name][:, k:k + n]
 
     def sm(name, n=8):
         return T.fs[:, SMALL[name]:SMALL[name] + n]
 
+    def sm1(name, k):
+        return T.fs[:, SMALL[name] + k:SMALL[name] + k + 1]
+
+    def blk(name, t, w=128):
+        return T[name][:, w * t:w * t + w]
+
     PS = [T["p%d" % k] for k in range(8)]
-    M4 = ["M%d" % t for t in range(4)]
-    H4 = ["H%d" % t for t in range(4)]
-    N4 = ["N%d" % t for t in range(4)]
-    X4 = ["X%d" % t for t in range(4)]
-    PI, PF = T.pi, T.pf
-    pf = lambda k: PF[:, k:k + 1]
+    M4, H4, N4, X4 = [["%s%d" % (n, t) for t in range(4)] for n in "MHNX"]
+    OX = ["ox%d" % k for k in range(8)]
+    FWALL = ["fw%d" % s for s in range(8)]
+    pf = lambda k: T.pf[:, k:k + 1]
 
     for m in range(8):
         for q in range(8):
@@ -180,26 +142,32 @@ def rank_program(g, core, T, topo):
     dma("y", "dw", T.wps[:], T.ws[:], [], ["wps"])
     for i in range(16):
         dma("y", "da", T.cwi[i:128:16, :], T.ar[:], [], ["cwi%d" % i])
-    dma("y", "du", T.ui[:], T.u[:], [], ["ui"])
+    for m in range(8):
+        dma("y", "du", T.ui[:, 8 * m:8 * m + 8], T.u[:, 64 * m:64 * m + 8], [], ["ui%d" % m])
+    dma("y", "du", T.ui[:, 64:512], T.u[:, 0:448], [], ["ui8"])
     dma("y", "dv", T.vi[:], T.v[:], [], ["vi"])
 
-    iota(PI[:, 9:10], [[0, 1]], 0, 1, ["pi9"], False)
-    iota(T.cf[:, 0:20], [[2, 10], [0, 2]], 0, 0, ["cf0"], True)
-    iota(T.cf[:, 32:40], [[16, 4], [64, 2]], 0, 0, ["cf1"], True)
-    iota(T.cf[:, 64:128], [[32, 2], [64, 2], [1, 16]], 0, 0, ["cf4"], True)
+    iota(col("pi", 9), [[0, 1]], 0, 1, ["pi9"], False)
+    iota(col("cf", 0, 20), [[2, 10], [0, 2]], 0, 0, ["cf0"], True)
+    iota(col("cf", 32, 8), [[16, 4], [64, 2]], 0, 0, ["cf1"], True)
+    iota(col("cf", 64, 64), [[32, 2], [64, 2], [1, 16]], 0, 0, ["cf4"], True)
     iota(T.nat[:], [[1, 320]], 0, 0, ["nat"], True)
     iota(T.zt[:], [[0, 512]], 0, 0, ["zt"], True)
     for b in range(4):
-        op("p", lambda b=b: g.affine_select(T.ce[:, 512 * b:512 * b + 512], T.zt[:], [[-1, 512]], Op.not_equal, 1.0, b, 4), ["zt"], ["ce%d" % b])
-    iota(T.ci[:, 0:128], [[-1, 128]], 128, 1, ["cia"], False)
-    iota(T.ci[:, 128:136], [[-16, 8]], 0, 1, ["cib"], False)
-    iota(T.cf[:, 56:58], [[-128, 2]], 128, 0, ["cf3"], True)
-    for col, sh, an in ((0, 0, 15), (1, 4, 1), (2, 5, 3), (4, 0, 1), (5, 1, 1), (6, 2, 1), (7, 0, 7), (8, 3, 1)):
-        ts(PI[:, col:col + 1], PI[:, 9:10], sh, Op.logical_shift_right, ["pi9"], ["pi%d" % col], an, Op.bitwise_and)
-    ts(PI[:, 3:4], PI[:, 9:10], 4, Op.logical_shift_right, ["pi9"], ["pi3"])
-    cp(PF[:, 0:10], PI[:, 0:10], ["pi%d" % k for k in range(10)], ["pf"])
+        select(blk("ce", b, 512), T.zt[:], [[-1, 512]], Op.not_equal, 1.0, b, 4, ["zt"], ["ce%d" % b])
+    iota(col("ci", 0, 128), [[-1, 128]], 128, 1, ["cia"], False)
+    iota(col("ci", 128, 8), [[-16, 8]], 0, 1, ["cib"], False)
+    iota(col("cf", 56, 2), [[-16, 2]], 16, 0, ["cf3"], True)
+    iota(T.k20[:], [[20, 4], [0, 8]], 0, 0, ["k20"], False)
+    iota(T.nat512[:], [[512, 320]], 0, 0, ["nat512"], True)
+    select(T.idb[:], blk("zt", 0), [[-1, 128]], Op.not_equal, 1.0, 0, 1, ["zt"], ["idb"])
+    select(T.tril[:], blk("zt", 0), [[1, 128]], Op.is_ge, 1.0, 0, -1, ["zt"], ["tril"])
+    for k, sh, an in ((0, 0, 15), (1, 4, 1), (2, 5, 3), (4, 0, 1), (5, 1, 1), (6, 2, 1), (7, 0, 7), (8, 3, 1)):
+        ts(col("pi", k), col("pi", 9), sh, Op.logical_shift_right, ["pi9"], ["pi%d" % k], an, Op.bitwise_and)
+    ts(col("pi", 3), col("pi", 9), 4, Op.logical_shift_right, ["pi9"], ["pi3"])
+    cp(col("pf", 0, 10), col("pi", 0, 10), ["pi%d" % k for k in range(10)], ["pf"])
     fill(T.b2[:], 0.0, ["b2"])
-    ts(T.ly[:], T.cf[:, 0:20], pf(1), Op.add, ["cf0", "pf"], ["ly"])
+    ts(T.ly[:], col("cf", 0, 20), pf(1), Op.add, ["cf0", "pf"], ["ly"])
     ts(pf(10), pf(1), 64.0, Op.mult, ["pf"], ["pf10"], pf(0), Op.add)
     ts(pf(11), pf(1), 16.0, Op.mult, ["pf"], ["pf11"])
     ts(pf(12), pf(2), 128.0, Op.mult, ["pf"], ["pf12"], pf(0), Op.add)
@@ -207,286 +175,289 @@ def rank_program(g, core, T, topo):
     ts(pf(15), pf(5), 4.0, Op.mult, ["pf"], ["pf15"], pf(4), Op.add)
     tt(pf(14), pf(13), pf(1), Op.mult, ["pf13", "pf"], ["pf14"])
     tt(pf(16), pf(15), pf(6), Op.add, ["pf15", "pf"], ["pf16"])
-    ts(T.lr[:], T.cf[:, 32:40], pf(12), Op.add, ["cf1", "pf12"], ["lr"])
-    ts(pf(17), pf(16), pf(4), Op.add, ["pf16", "pf"], ["pf17"], pf(14), Op.add)
-    ts(pf(18), pf(16), pf(6), Op.add, ["pf16", "pf"], ["pf18"], pf(14), Op.subtract)
-    ts(T.ox[:, 0:64], T.cf[:, 64:128], pf(11), Op.add, ["cf4", "pf11"], ["ox0"])
-    ts(T.pk[:, 0:1], pf(17), 16.0, Op.mult, ["pf17"], ["pk0"])
-    ts(T.pk[:, 2:3], pf(18), 16.0, Op.mult, ["pf18"], ["pk1"])
-    ts(T.l0[:], T.nat[:, 0:4], 16.0, Op.mult, ["nat", "pf10"], ["l0"], pf(10), Op.add)
+    ts(T.lr[:], col("cf", 32, 8), pf(12), Op.add, ["cf1", "pf12"], ["lr"])
+    ts(pf(24), pf(2), 3.0, Op.is_lt, ["pf"], ["pf24"], 64.0, Op.mult)
+    ts(pf(25), pf(24), pf(12), Op.add, ["pf24", "pf12"], ["pf25"])
+    ts(T.lr7[:, 0:8:2], T.cf[:, 32:40:2], pf(12), Op.add, ["cf1", "pf12"], ["lr7_"])
+    ts(T.lr7[:, 1:8:2], T.cf[:, 32:40:2], pf(25), Op.add, ["cf1", "pf25", "lr7_"], ["lr7"])
+    ts(pf(26), pf(3), 7.0, Op.is_equal, ["pf"], ["pf26"], 128.0, Op.mult)
+    ts(pf(17), pf(16), pf(4), Op.add, ["pf16", "pf14", "pf"], ["pf17"], pf(14), Op.add)
+    ts(pf(23), pf(16), pf(6), Op.add, ["pf16", "pf14", "pf"], ["pf23"], pf(14), Op.subtract)
+    ts(pf(18), pf(23), 16.0, Op.mult, ["pf23"], ["pf18"])
+    ts(col("ox", 0, 64), col("cf", 64, 64), pf(11), Op.add, ["cf4", "pf11"], ["ox0"])
+    ts(col("pk", 0), pf(17), 16.0, Op.mult, ["pf17", "pf26"], ["pk0"], pf(26), Op.add)
+    ts(col("pk", 2, 2), col("cf", 0, 2), 0.0, Op.mult, ["cf0", "pf18"], ["pk1"], pf(18), Op.add)
+    ts(T.l0[:], col("nat", 0, 4), 16.0, Op.mult, ["nat", "pf10"], ["l0"], pf(10), Op.add)
     fill(T.b1[:], 0.0, ["b1"])
     fill(T.ca[:], 0.0, ["ca"])
+    fill(T.cb[:], 0.0, ["cb"])
 
-    def step_a(s):
-        lst, key = (T.l0[:], "l0") if s == 0 else (T.of[:, 4 * s - 4:4 * s], "of%d" % (s - 1))
-        cp(T.ox[:, 64 * s + 64:64 * s + 128], T.fw[:, 320 * (8 - s):320 * (8 - s) + 320].indirect(lst), ["fw%d" % s, key], ["ox%d" % (s + 1)])
-
-    def step_b(s):
-        tr(T.tt[:, 64 * s:64 * s + 64], T.ox[:, 64 * s + 64:64 * s + 128], ["ox%d" % (s + 1)], ["tt%d" % s])
-
-    def step_c(s):
-        cp(T.of[:, 4 * s:4 * s + 4], T.tt[:, 64 * s:64 * s + 64:16], ["tt%d" % s], ["of%d" % s])
-
-    FWALL = ["fw%d" % s for s in range(8)]
+    def step(s):
+        if s == 7:
+            cp(T.o7[:], col("fw", 320, 320).indirect(col("of", 24, 8)), ["fw7", "of6"], ["o7"])
+            tr(col("tl", 128, 128), T.o7[:], ["o7"], ["tl7"])
+            return
+        lst, key = (T.l0[:], "l0") if s == 0 else (blk("of", s - 1, 4), "of%d" % (s - 1))
+        cp(blk("ox", s + 1, 64), blk("fw", 8 - s, 320).indirect(lst), ["fw%d" % s, key], [OX[s + 1]])
+        tr(blk("tt", s, 64), blk("ox", s + 1, 64), [OX[s + 1]], ["tt%d" % s])
+        cp(col("of", 24, 8) if s == 6 else blk("of", s, 4), T.tt[:, 64 * s:64 * s + 64:8 if s == 6 else 16], ["tt%d" % s], ["of%d" % s])
 
     def places():
-        cp(T.rl[:], T.ox[:, 64:576].indirect(T.lr[:]), ["ox%d" % k for k in range(1, 9)] + ["lr"], ["rl"])
-        tr(T.tl[:], T.rl[:], ["rl"], ["tl"])
-        cp(T.lw[:], T.tl[:].indirect(T.pk[:, 0:1]), ["tl", "pk0"], ["lw"])
+        cp(T.rl[:], col("ox", 64, 448).indirect(T.lr7[:]), OX[1:] + ["lr7"], ["rl"])
+        tr(col("tl", 0, 128), T.rl[:], ["rl"], ["tl"])
+        cp(T.lw[:], T.tl[:].indirect(col("pk", 0)), ["tl", "tl7", "pk0"], ["lw"])
 
-    def decode_x():
+    def decode(name, keys, w, q, s, key, scale, view=None):
         for t in range(4):
-            mm(PS[t][:, 0:320], T.qe[:, 128 * t:128 * t + 128], T.se[:, 128 * t:128 * t + 128], T.qx[:], T.sx[:], ["qe", "qx"], ["#%d" % t])
+            mm(PS[t][:, 0:w], blk("qe", t), blk("se", t), q, s, ["qe", key], ["#%d" % t])
         for t in range(4):
-            act(T.fh[:, 320 * t:320 * t + 320], PS[t][:, 0:320], ["#%d" % t], ["fh%d" % t], scale=0.5)
+            times(T[name][:, t:4 * w:4] if view else blk(name, t, w), PS[t][:, 0:w], ["#%d" % t], [keys[t]], scale)
 
-    def base_x():
-        for t in range(4):
-            act(T.xt[:, t:1280:4], T.fh[:, 320 * t:320 * t + 320], ["fh%d" % t], [X4[t]], scale=2.0)
+    FH4, DH4 = ["fh%d" % t for t in range(4)], ["dh%d" % t for t in range(4)]
+    LW = col("lw", 0, 8)
 
-    def spread(m):
-        act(T.yb[:, 320 * m:320 * m + 320], T.mwf[:, 24 * m:24 * m + 20].indirect(T.ly[:]), ["mwf%d" % m, "ly"], ["yb%d" % m])
-
-    def turn(m):
-        tr(T.fw[:, 320 * (8 - m):320 * (8 - m) + 320], T.yb[:, 320 * m:320 * m + 320], ["yb%d" % m], ["fw%d" % m])
-
-    def unpack(m):
-        cp(T.mwf[:, 24 * m:24 * m + 20], T.mwi[:, 24 * m:24 * m + 20], ["mwi%d.%d" % (m, q) for q in range(8)], ["mwf%d" % m])
-
-    unpack(0)
-    spread(0)
-    unpack(1)
-    spread(1)
-    unpack(2)
-    spread(2)
-    turn(0)
-    step_a(0)
-    turn(1)
-    for s in range(7):
-        step_b(s)
-        if s + 3 < 8:
-            unpack(s + 3)
-            spread(s + 3)
-        step_c(s)
-        if s == 1:
-            fill(T.cb[:], 0.0, ["cb"])
-        elif s == 2:
-            quant(T.qx[:], T.sx[:], T.xi[:], ["xi"], ["qx"])
-        elif s == 3:
-            quant(T.qe[:], T.se[:], T.ce[:], ["ce%d" % t for t in range(4)], ["qe"])
-        elif s == 4:
-            decode_x()
-        step_a(s + 1)
-        if s + 2 < 8:
-            turn(s + 2)
+    for m in range(8):
+        cp(col("mwf", 24 * m, 20), col("mwi", 24 * m, 20), ["mwi%d.%d" % (m, q) for q in range(8)], ["mwf%d" % m])
+        times(blk("yb", m, 320), col("mwf", 24 * m, 20).indirect(T.ly[:]), ["mwf%d" % m, "ly"], ["yb%d" % m], 1.0)
+        tr(blk("fw", 8 - m, 320), blk("yb", m, 320), ["yb%d" % m], ["fw%d" % m])
+        step(m)
+    quant(T.qx[:], T.sx[:], T.xi[:], ["xi"], ["qx"])
+    quant(T.qe[:], T.se[:], T.ce[:], ["ce%d" % t for t in range(4)], ["qe"])
+    decode("fh", FH4, 320, T.qx[:], T.sx[:], "qx", 0.5)
     places()
 
-    def more_constants():
-        ts(T.idb[:], T.ci[:, 0:128], 128.0, Op.is_equal, ["cia"], ["idb"])
-        for t in range(5):
-            fill(T.fs[:, SMALL["sc"] + t:SMALL["sc"] + t + 1], 32.0 ** -t, ["sc%d" % t])
-        fill(T.fs[:, SMALL["sc"] + 5:SMALL["sc"] + 6], 0.0, ["sc5"])
-        ts(T.cj[:, 0:128], T.ci[:, 0:128], 15, Op.bitwise_and, ["cia"], ["cja"])
-        ts(T.cj[:, 128:136], T.ci[:, 128:136], 4, Op.arith_shift_right, ["cib"], ["cjb"])
-        ts(T.mod[:], T.cj[:, 0:128], 0.0, Op.is_equal, ["cja"], ["mod"])
-        ts(T.m8[:], T.cj[:, 128:136], 0.0, Op.is_equal, ["cjb"], ["m8"])
-        ts(T.tril[:], T.ci[:, 0:128], 128.0, Op.is_gt, ["cia"], ["tril"])
-        for t in range(3):
-            ts(T.ca[:, 512 * t + t:512 * t + 512:4], T.mod[:], 0.0, Op.mult, ["mod", "ca"], ["ca.%d" % t], 32.0 ** t, Op.add)
-            ts(T.cb[:, 512 * t + t:512 * t + 512:4], T.mod[:], 32.0 ** t, Op.mult, ["mod", "cb"], ["cb.%d" % t])
-        quant(T.qa[:], T.sa[:], T.ca[:], ["ca"] + ["ca.%d" % t for t in range(3)], ["qa"])
-        quant(T.qb[:], T.sb[:], T.cb[:], ["cb"] + ["cb.%d" % t for t in range(3)], ["qb"])
-        quant(T.qu[:], T.su[:], T.ui[:], ["ui"], ["qu"])
-        ts(sm("jw"), T.nat[:, 0:8], 16.0, Op.mult, ["nat", "pf"], ["jw"], pf(0), Op.add)
-        ts(pf(19), pf(7), 16.0, Op.mult, ["pf"], ["pf19"])
-        ts(pf(20), pf(8), -128.0, Op.mult, ["pf"], ["pf20"], 129.0, Op.add)
-        ts(sm("jd"), sm("jw"), 320.0, Op.add, ["jw"], ["jd"])
-        ts(T.nat512[:], T.nat[:], 512.0, Op.mult, ["nat"], ["nat512"])
-        ts(T.yy[:, 32:33], pf(9), 1024.0, Op.mult, ["pf"], ["yyc"])
-        ts(T.la[:, 0:2], T.cf[:, 56:58], pf(19), Op.add, ["cf3", "pf19"], ["la0"])
-        tt(pf(21), pf(20), pf(19), Op.add, ["pf20", "pf19"], ["pf21"])
-        ts(T.la[:, 2:4], T.nat[:, 0:2], 0.0, Op.mult, ["nat", "pf21"], ["la1"], pf(21), Op.add)
+    for t in range(5):
+        fill(sm1("sc", t), 32.0 ** -t, ["sc%d" % t])
+    fill(sm1("sc", 5), 0.0, ["sc5"])
+    ts(col("cj", 0, 128), col("ci", 0, 128), 15, Op.bitwise_and, ["cia"], ["cja"])
+    ts(col("cj", 128, 8), col("ci", 128, 8), 4, Op.arith_shift_right, ["cib"], ["cjb"])
+    ts(T.mod[:], col("cj", 0, 128), 0.0, Op.is_equal, ["cja"], ["mod"])
+    ts(T.m8[:], col("cj", 128, 8), 0.0, Op.is_equal, ["cjb"], ["m8"])
+    for t in range(3):
+        ts(T.ca[:, 512 * t + t:512 * t + 512:4], T.mod[:], 0.0, Op.mult, ["mod", "ca"], ["ca.%d" % t], 32.0 ** t, Op.add)
+        ts(T.cb[:, 512 * t + t:512 * t + 512:4], T.mod[:], 32.0 ** t, Op.mult, ["mod", "cb"], ["cb.%d" % t])
+    quant(T.qa[:], T.sa[:], T.ca[:], ["ca"] + ["ca.%d" % t for t in range(3)], ["qa"])
+    quant(T.qb[:], T.sb[:], T.cb[:], ["cb"] + ["cb.%d" % t for t in range(3)], ["qb"])
+    quant(T.qu[:], T.su[:], T.ui[:], ["ui%d" % m for m in range(9)], ["qu"])
+    quant(T.qv[:], T.sv[:], T.vi[:], ["vi"], ["qv"])
+    ts(sm("jw"), col("nat", 0, 8), 16.0, Op.mult, ["nat", "pf"], ["jw"], pf(0), Op.add)
+    ts(pf(19), pf(7), 2.0, Op.mult, ["pf"], ["pf19"])
+    ts(pf(20), pf(8), -16.0, Op.mult, ["pf"], ["pf20"], 17.0, Op.add)
+    ts(sm("jd"), sm("jw"), 4.0, Op.mult, ["jw"], ["jd"], 1280.0, Op.add)
+    ts(col("yy", 32), pf(9), 1024.0, Op.mult, ["pf"], ["yyc"])
+    ts(col("la", 0, 2), col("cf", 56, 2), pf(19), Op.add, ["cf3", "pf19"], ["la0"])
+    tt(pf(21), pf(20), pf(19), Op.add, ["pf20", "pf19"], ["pf21"])
+    ts(col("la", 2, 2), col("nat", 0, 2), 0.0, Op.mult, ["nat", "pf21"], ["la1"], pf(21), Op.add)
+    cp(T.cwf[:], T.cwi[:], ["cwi%d" % i for i in range(16)], ["cwf"])
+    ts(pf(22), pf(3), -327680.0, Op.mult, ["pf"], ["pf22"], 2621440.0, Op.add)
 
-    def candidates_a():
-        cp(T.rle[:], T.ox[:, 0:512].indirect(T.lr[:]), ["ox%d" % k for k in range(8)] + ["lr"], ["rle"])
-        tr(T.te[:], T.rle[:], ["rle"], ["te"])
-        cp(T.ew[:], T.te[:].indirect(T.pk[:, 2:3]), ["te", "pk1"], ["ew"])
-        ts(T.e1[:], T.ew[:, 0:8], 15, Op.bitwise_and, ["ew"], ["e1"])
-        ts(T.e2[:], T.ew[:, 0:8], 4, Op.logical_shift_right, ["ew"], ["e2"])
-        cp(T.el[:], T.ew[:, 0:8], ["ew"], ["el"])
-        ts(T.ec[:], T.e1[:], 80.0, Op.mult, ["e1"], ["ec"])
-        tt(T.e1[:], T.ec[:], T.e2[:], Op.add, ["ec", "e2"], ["e1"])
-        for k in range(4):
-            ts(T.lc[:, 8 * k:8 * k + 8], T.e1[:], 20.0 * k, Op.add, ["e1"], ["lc%d" % k])
-
-    def candidates_b():
-        act(T.rf[:, 4:768:6], T.nat[:].indirect(T.lw[:, 0:8]), ["nat", "lw"], ["rf4"])
-        act(T.rf[:, 5:768:6], T.nat[:].indirect(T.el[:]), ["nat", "el", "pf22"], ["rf5"], func=Act.Identity, scale=1024.0, bias=pf(22))
-        for k in range(4):
-            act(T.rf[:, k:768:6], T.cwf[:].indirect(T.lc[:, 8 * k:8 * k + 8]), ["cwf", "lc%d" % k], ["rf%d" % k])
-        for gr in range(8):
-            dma("y", "dc", T.cp[:, 6 * gr:6 * gr + 6], T.rf[16 * gr:16 * gr + 1, 0:768], ["rf%d" % k for k in range(6)], ["cp%d" % gr])
-
-    def candidates_c():
-        C = ["cp%d" % k for k in range(8)]
-        for k in range(4):
-            tt(T.ne[:, 8 * k:8 * k + 8], T.cp[:, k:48:6], T.cp[:, 4:48:6], Op.not_equal, C, ["ne%d" % k])
-            tt(T.sk[:, 8 * k:8 * k + 8], T.cp[:, k:48:6], T.cp[:, 5:48:6], Op.add, C, ["sk%d" % k])
-        tt(T.pp[:], T.ne[:], T.sk[:], Op.mult, ["ne%d" % k for k in range(4)] + ["sk%d" % k for k in range(4)], ["pp"])
-
-    def make_h(k, wc, wp, wkeys, mc, mp, mkey, engines):
-        for b in range(4):
-            c = slice(128 * b, 128 * b + 128)
-            mm(PS[b][:, 0:128], wc[:, c], wp[:, c], mc[:], mp[:], wkeys + [mkey], ["#%d" % b])
-        for b in range(4):
-            if engines[b] == "s":
-                act(T.ht[:, b:512:4], PS[b][:, 0:128], ["#%d" % b], [H4[b]], func=Act.Relu, scale=0.03125)
-            else:
-                ts(T.ht[:, b:512:4], PS[b][:, 0:128], 0.0, Op.max, ["#%d" % b], [H4[b]], 0.03125, Op.mult)
-        quant(T["qh%d" % k][:], T["sh%d" % k][:], T.ht[:], H4, ["qh%d" % k])
-
-    def state_lists():
-        tt(sm("wn"), sm("fi"), sm("jw"), Op.is_equal, ["fi%d" % c for c in range(8)] + ["jw"], ["wn"])
-        ts(sm("xd"), sm("nl"), -1.0 / 512, Op.mult, ["nl"], ["xd"])
-        tt(sm("xd"), sm("xd"), sm("jd"), Op.subtract, ["xd", "jd"], ["xd"])
-        tt(sm("xd"), sm("xd"), sm("wn"), Op.mult, ["xd", "wn"], ["xd"])
-        tt(sm("xd"), sm("xd"), sm("jd"), Op.add, ["xd", "jd"], ["xd"])
-        for t in range(4):
-            ts(T.xl[:, 8 * t:8 * t + 8], sm("xd"), 4.0, Op.mult, ["xd"], ["xl%d" % t], float(t), Op.add)
-
-    def scatter_state():
-        for t in range(4):
-            cp(T.xt[:].indirect(T.xl[:, 8 * t:8 * t + 8]), T.nt[:, t:512:4], ["xl%d" % t, N4[t]], X4)
-        quant(T.qx[:], T.sx[:], T.xt[:, 0:1280], X4, ["qx"])
-
+    heir = T.cores[(r - STEP[2]) % N]
+    send([(T.wdp[:], T.wps[:])], heir, "aw", ["wps"])
     for k in range(3):
         donor, client = T.cores[(r + STEP[k]) % N], T.cores[(r - STEP[k]) % N]
-        qm, sm_, qh, sh = T["qm%d" % k], T["sm%d" % k], T["qh%d" % k], T["sh%d" % k]
+        qm, sp, qh, sh = [T["%s%d" % (n, k)] for n in ("qm", "sm", "qh", "sh")]
         if k == 0:
             for t in range(4):
-                src = T.fh[:, 320 * t:320 * t + 320].indirect(T.lw[:, 0:8])
-                if t % 2 == 0:
-                    act(T.mt[:, t:512:4], src, ["fh%d" % t, "lw"], [M4[t]], scale=2.0)
-                else:
-                    ts(T.mt[:, t:512:4], src, 2.0, Op.mult, ["fh%d" % t, "lw"], [M4[t]])
+                times(T.mt[:, t:512:4], blk("fh", t, 320).indirect(LW), [FH4[t], "lw"], [M4[t]], 2.0)
         else:
             quant(T.qn[:], T.sn[:], T.nt[:], N4, ["qn"])
-            for t in range(4):
-                mm(PS[t][:, 0:128], T.qe[:, 128 * t:128 * t + 128], T.se[:, 128 * t:128 * t + 128], T.qn[:], T.sn[:], ["qe", "qn"], ["#%d" % t])
-            if k == 2:
-                candidates_a()
-            for t in range(4):
-                if t % 2 == 0:
-                    act(T.mt[:, t:512:4], PS[t][:, 0:128], ["#%d" % t], [M4[t]])
-                else:
-                    cp(T.mt[:, t:512:4], PS[t][:, 0:128], ["#%d" % t], [M4[t]])
-        quant(qm[:], sm_[:], T.mt[:], M4, ["qm%d" % k])
-        if k == 0:
-            dst = T.cores[(r - STEP[2]) % N]
-            send([(T.wdc[:].bitcast(B8), T.wcs[:].bitcast(B8)), (T.wdp[:], T.wps[:])], dst, "aw", ["wcs", "wps"])
-            arrives("aw", T.cores[(r + STEP[2]) % N], ["wd"])
+            decode("mt", M4, 128, T.qn[:], T.sn[:], "qn", 1.0, True)
+        quant(qm[:], sp[:], T.mt[:], M4, ["qm%d" % k])
+        mc, mp, mkey, wc, wp, wkeys = qm, sp, "qm%d" % k, T.wdc, T.wdp, ["wd"]
+        hc, hp, hkey = qh, sh, "qh%d" % k
         if k < 2:
-            send([(T["mc%d" % k][:].bitcast(B8), qm[:].bitcast(B8)), (T["mp_%d" % k][:], sm_[:])], donor, "am%d" % k, ["qm%d" % k])
-            arrives("am%d" % k, client, ["mc%d" % k])
-            if k == 0:
-                cp(T.cwf[:], T.cwi[:], ["cwi%d" % i for i in range(16)], ["cwf"])
-                ts(pf(22), pf(3), -327680.0, Op.mult, ["pf"], ["pf22"], 2621440.0, Op.add)
-            candidates_a()
-            candidates_b()
-            make_h(k, T.wcs, T.wps, ["wcs", "wps"], T["mc%d" % k], T["mp_%d" % k], "mc%d" % k, "svsv")
+            send([(T["mc%d" % k][:].bitcast(B8), qm[:].bitcast(B8)), (T["mp_%d" % k][:], sp[:])], donor, "am%d" % k, ["qm%d" % k])
+            mc, mp, mkey, wc, wp, wkeys = T["mc%d" % k], T["mp_%d" % k], "mc%d" % k, T.wcs, T.wps, ["wcs", "wps"]
+            arrives("am%d" % k, client, [mkey])
+        for b in range(4):
+            mm(PS[b][:, 0:128], wc[:, 128 * b:128 * b + 128], wp[:, 128 * b:128 * b + 128], mc[:], mp[:], wkeys + [mkey], ["#%d" % b])
+        for b in range(4):
+            o, i = T.ht[:, b:512:4], PS[b][:, 0:128]
+            op("vs", lambda e, o=o, i=i: V.tensor_scalar(o, i, 0.0, 0.03125, Op.max, Op.mult) if e == "v" else S.activation(o, i, Act.Relu, scale=0.03125), ["#%d" % b], [H4[b]])
+        quant(qh[:], sh[:], T.ht[:], H4, ["qh%d" % k])
+        if k < 2:
             send([(T["hc%d" % k][:].bitcast(B8), qh[:].bitcast(B8)), (T["hp%d" % k][:], sh[:])], client, "ah%d" % k, ["qh%d" % k])
-            arrives("ah%d" % k, donor, ["hc%d" % k])
             hc, hp, hkey = T["hc%d" % k], T["hp%d" % k], "hc%d" % k
-        else:
-            candidates_b()
-            make_h(k, T.wdc, T.wdp, ["wd"], qm, sm_, "qm2", "vvvv")
-            hc, hp, hkey = qh, sh, "qh2"
+            arrives("ah%d" % k, donor, [hkey])
+            if k == 0:
+                send([(T.wdc[:].bitcast(B8), T.wcs[:].bitcast(B8))], heir, "aw", ["wcs"])
+                arrives("aw", T.cores[(r + STEP[2]) % N], ["wd"])
+        cp(T.rle[:], T.ox[:].indirect(T.lr[:]), OX + ["lr"], ["rle"])
+        tr(T.te[:], T.rle[:], ["rle"], ["te"])
+        cp(T.ew[:], T.te[:].indirect(col("pk", 2, 2)), ["te", "pk1"], ["ew"])
+        ts(T.e1[:], T.ew[:], 15, Op.bitwise_and, ["ew"], ["e1"])
+        ts(T.e2[:], T.ew[:], 4, Op.logical_shift_right, ["ew"], ["e2"])
+        cp(T.el[:], col("ew", 0, 8), ["ew"], ["el"])
+        ts(T.e3[:], T.e1[:], 80.0, Op.mult, ["e1"], ["e3"])
+        tt(T.ec[:], T.e2[:], T.k20[:], Op.add, ["e2", "k20"], ["ec"])
+        tt(T.e1[:], T.e3[:], T.ec[:], Op.add, ["e3", "ec"], ["e1"])
+        cp(T.lc[:], T.e1[:], ["e1"], ["lc"])
+        times(T.rf[:, 4:768:6], T.nat[:].indirect(LW), ["nat", "lw"], ["rf4"], 1.0)
+        op("s", lambda _: S.activation(T.rf[:, 5:768:6], T.nat[:].indirect(T.el[:]), Act.Identity, scale=1024.0, bias=pf(22)), ["nat", "el", "pf22"], ["rf5"])
+        for q in range(4):
+            times(T.rf[:, q:768:6], T.cwf[:].indirect(blk("lc", q, 8)), ["cwf", "lc"], ["rf%d" % q], 1.0)
+        for m in range(8):
+            dma("y", "dc", blk("cp", m, 6), T.rf[16 * m:16 * m + 1, 0:768], ["rf%d" % q for q in range(6)], ["cp%d" % m], k)
+        C = ["cp%d" % m for m in range(8)]
+        for q in range(4):
+            tt(blk("ne", q, 8), T.cp[:, q:48:6], T.cp[:, 4:48:6], Op.not_equal, C, ["ne%d" % q])
+            tt(blk("sk", q, 8), T.cp[:, q:48:6], T.cp[:, 5:48:6], Op.add, C, ["sk%d" % q])
+        tt(T.pp[:], T.ne[:], T.sk[:], Op.mult, ["ne%d" % q for q in range(4)] + ["sk%d" % q for q in range(4)], ["pp"])
         if k:
-            scatter_state()
-            decode_x()
-        else:
-            more_constants()
-        candidates_c()
-        mm(PS[4][:, 0:128], hc[:], hp[:], T.qu[:], T.su[:], [hkey, "qu"], ["#4"])
+            for t in range(4):
+                cp(T.xt[:].indirect(blk("xl", t, 8)), T.nt[:, t:512:4], ["xl%d" % t, N4[t]], X4)
+            quant(T.qx[:], T.sx[:], col("xt", 0, 1280), X4, ["qx"])
+            decode("fh", FH4, 320, T.qx[:], T.sx[:], "qx", 0.5)
         for t in range(4):
-            mm(PS[t][:, 0:128], T.qe[:, 128 * t:128 * t + 128], T.se[:, 128 * t:128 * t + 128], hc[:], hp[:], ["qe", hkey], ["#%d" % t])
-        ts(T.sg[:, 0:128], PS[4][:, 0:128], 0.0, Op.is_gt, ["#4"], ["sg0"])
-        ts(T.sg[:, 128:256], PS[4][:, 0:128], 0.0, Op.is_le, ["#4"], ["sg1"])
-        tt(T.xx[:], T.sg[:].indirect(T.la[:, 0:2]), T.pp[:], Op.mult, ["sg0", "sg1", "la0", "pp"], ["xx"])
-        tt(T.yy[:, 0:32], T.sg[:].indirect(T.la[:, 2:4]), T.xx[:], Op.mult, ["sg0", "sg1", "la1", "xx"], ["yy"])
-        red(sm("rq", 1), T.yy[:, 0:33], Op.max, ["yy", "yyc"], ["rq"])
-        ts(T.qd[:, 0:6], sm("sc", 6), sm("rq", 1), Op.mult, ["rq"] + ["sc%d" % t for t in range(6)], ["qd"])
-        ts(sm("nq", 5), T.qd[:, 1:6], -32.0, Op.mult, ["qd"], ["nq"])
-        tt(sm("dg", 5), sm("nq", 5), T.qd[:, 0:5], Op.add, ["nq", "qd"], ["dg"])
-        dg = lambda t: T.fs[:, SMALL["dg"] + t:SMALL["dg"] + t + 1]
+            times(T.xt[:, t:1280:4], blk("fh", t, 320), [FH4[t]], [X4[t]], 2.0)
+        mm(PS[4][:, 0:128], hc[:], hp[:], T.qu[:], T.su[:], [hkey, "qu"], ["#4"])
+        ts(col("sg", 0, 16), PS[4][:, 0:16], 0.0, Op.is_gt, ["#4"], ["sg0"])
+        ts(col("sg", 16, 16), PS[4][:, 0:16], 0.0, Op.is_le, ["#4"], ["sg1"])
+        tt(T.xx[:], T.sg[:].indirect(col("la", 0, 2)), T.pp[:], Op.mult, ["sg0", "sg1", "la0", "pp"], ["xx"])
+        tt(col("yy", 0, 32), T.sg[:].indirect(col("la", 2, 2)), T.xx[:], Op.mult, ["sg0", "sg1", "la1", "xx"], ["yy"])
+        red(sm("rq", 1), col("yy", 0, 33), Op.max, ["yy", "yyc"], ["rq"])
+        ts(col("qd", 0, 6), sm("sc", 6), sm("rq", 1), Op.mult, ["rq"] + ["sc%d" % t for t in range(6)], ["qd"])
+        ts(sm("nq", 5), col("qd", 1, 5), -32.0, Op.mult, ["qd"], ["nq"])
+        tt(sm("dg", 5), sm("nq", 5), col("qd", 0, 5), Op.add, ["nq", "qd"], ["dg"])
         for t in range(3):
-            ts(T.b1[:, t:512:4], T.idb[:], dg(2 + t), Op.mult, ["idb", "dg", "b1"], ["ba%d" % t])
-        quant(T.qk[:, 0:128], T.sk1[:, 0:128], T.b1[:, 0:512], ["ba%d" % t for t in range(3)] + ["b1"], ["qk0"])
+            times(T.b1[:, t:512:4], T.idb[:], ["idb", "dg", "b1"], ["ba%d" % t], sm1("dg", 2 + t))
+        quant(blk("qk", 0), blk("sk1", 0), col("b1", 0, 512), ["ba%d" % t for t in range(3)] + ["b1"], ["qk0"])
         for t in range(3):
-            mm(PS[5][:, 0:128], T.qa[:, 128 * t:128 * t + 128], T.sa[:, 128 * t:128 * t + 128], T.qk[:, 0:128], T.sk1[:, 0:128], ["qa", "qk0"], ["#5"], t == 0, t == 2)
+            mm(PS[5][:, 0:128], blk("qa", t), blk("sa", t), blk("qk", 0), blk("sk1", 0), ["qa", "qk0"], ["#5"], t == 0, t == 2)
         for t in range(2):
-            act(T.b1[:, 512 + t:1024:4], T.idb[:], ["idb", "dg", "b1"], ["bb%d" % t], scale=dg(t))
+            times(T.b1[:, 512 + t:1024:4], T.idb[:], ["idb", "dg", "b1"], ["bb%d" % t], sm1("dg", t))
         for t in range(3):
-            ts(T.b1[:, 1024 + t:1056:4], T.m8[:], dg(2 + t), Op.mult, ["m8", "dg", "b1"], ["bc%d" % t])
-        ts(sm("kf", 1), T.qd[:, 2:3], 1.0, Op.add, ["qd"], ["kf"])
-        quant(T.qk[:, 256:384], T.sk1[:, 256:384], T.b1[:, 1024:1536], ["bc0", "bc1", "bc2", "b1"], ["qk2"])
+            times(T.b1[:, 1024 + t:1056:4], T.m8[:], ["m8", "dg", "b1"], ["bc%d" % t], sm1("dg", 2 + t))
+        ts(sm("kf", 1), col("qd", 2), 1.0, Op.add, ["qd"], ["kf"])
+        quant(blk("qk", 2), blk("sk1", 2), col("b1", 1024, 512), ["bc0", "bc1", "bc2", "b1"], ["qk2"])
         for t in range(3):
-            mm(PS[7][:, 0:128], T.qb[:, 128 * t:128 * t + 128], T.sb[:, 128 * t:128 * t + 128], T.qk[:, 256:384], T.sk1[:, 256:384], ["qb", "qk2"], ["#7"], t == 0, t == 2)
-        act(sm("kw"), PS[7][:, 0:8], ["#7"], ["kw"])
+            mm(PS[7][:, 0:128], blk("qb", t), blk("sb", t), blk("qk", 2), blk("sk1", 2), ["qb", "qk2"], ["#7"], t == 0, t == 2)
+        times(sm("kw"), PS[7][:, 0:8], ["#7"], ["kw"], 1.0)
         ts(T.kt[:], T.tril[:], sm("kf", 1), Op.mult, ["tril", "kf"], ["kt"], -1.0, Op.add)
         tt(T.eq[:], PS[5][:, 0:128], T.kt[:], Op.is_equal, ["#5", "kt"], ["eq"])
         red(sm("lo", 1), T.eq[:], Op.max, ["eq"], ["lo"])
         ts(T.b2[:, 0:32:4], T.m8[:], sm("lo", 1), Op.mult, ["m8", "lo", "b2"], ["b2a"])
         quant(T.ql[:], T.sl[:], T.b2[:], ["b2", "b2a"], ["ql"])
-        mm(PS[4][:, 0:128], T.qb[:, 0:128], T.sb[:, 0:128], T.ql[:], T.sl[:], ["qb", "ql"], ["#4"])
-        quant(T.qk[:, 128:256], T.sk1[:, 128:256], T.b1[:, 512:1024], ["bb0", "bb1", "b1"], ["qk1"])
+        mm(PS[4][:, 0:128], blk("qb", 0), blk("sb", 0), T.ql[:], T.sl[:], ["qb", "ql"], ["#4"])
+        quant(blk("qk", 1), blk("sk1", 1), col("b1", 512, 512), ["bb0", "bb1", "b1"], ["qk1"])
         for t in range(2):
-            mm(PS[6][:, 0:128], T.qa[:, 128 * t:128 * t + 128], T.sa[:, 128 * t:128 * t + 128], T.qk[:, 128:256], T.sk1[:, 128:256], ["qa", "qk1"], ["#6"], t == 0, t == 1)
-        act(T.va[:], PS[6][:, 0:128], ["#6"], ["va"])
-        for t in range(4):
-            act(T.dh[:, 128 * t:128 * t + 128], PS[t][:, 0:128], ["#%d" % t], ["dh%d" % t], scale=0.5)
-        base_x()
+            mm(PS[6][:, 0:128], blk("qa", t), blk("sa", t), blk("qk", 1), blk("sk1", 1), ["qa", "qk1"], ["#6"], t == 0, t == 1)
+        times(T.va[:], PS[6][:, 0:128], ["#6"], ["va"], 1.0)
         tt(sm("dj"), sm("jw"), sm("kw"), Op.subtract, ["jw", "kw"], ["dj"])
         tt(sm("t1"), PS[4][:, 0:8], sm("dj"), Op.mult, ["#4", "dj"], ["t1"])
         tt(sm("t2"), sm("t1"), sm("kw"), Op.add, ["t1", "kw"], ["t2"])
         cp(T.ofs[:], sm("t2"), ["t2"], ["ofs"])
-        cp(T.fw[:].indirect(T.ofs[:]), T.va[:], ["ofs", "va"], FWALL + ["fwd"])
+        cp(T.fw[:].indirect(T.ofs[:]), T.va[:], ["ofs", "va"], FWALL)
+        decode("dh", DH4, 128, hc[:], hp[:], hkey, 0.5)
         if k == 2:
-            for gr in range(8):
-                dma("y", "do", T.fo[gr:gr + 1, :], T.fw[0:1, 320 * (8 - gr):320 * (8 - gr) + 320], ["fw%d" % gr], [])
+            for m in range(8):
+                dma("y", "do", T.fo[m:m + 1, :], T.fw[0:1, 320 * (8 - m):320 * (8 - m) + 320], ["fw%d" % m], [])
         for s in range(8):
-            step_a(s)
-            if s < 7:
-                step_b(s)
-                step_c(s)
+            step(s)
         places()
-        ts(sm("nl"), T.lw[:, 0:8], -512.0, Op.mult, ["lw"], ["nl"])
-        tt(T.kk[:], T.nat512[:].indirect(T.lw[:, 0:8]), T.nat[:, 0:128], Op.add, ["nat512", "lw", "nat"], ["kk"])
+        ts(sm("nl"), LW, -512.0, Op.mult, ["lw"], ["nl"])
+        tt(T.kk[:], T.nat512[:].indirect(LW), col("nat", 0, 128), Op.add, ["nat512", "lw", "nat"], ["kk"])
         for c in range(8):
-            d, b = T.dd[:, 128 * c:128 * c + 128], T.fs[:, SMALL["nl"] + c:SMALL["nl"] + c + 1]
-            if c in (0, 3, 6):
-                ts(d, T.kk[:], b, Op.add, ["kk", "nl"], ["dd%d" % c])
-            else:
-                act(d, T.kk[:], ["kk", "nl"], ["dd%d" % c], func=Act.Identity, bias=b)
-        for c in (0, 1, 3, 2, 6, 4, 5, 7):
-            red(T.fs[:, SMALL["fi"] + c:SMALL["fi"] + c + 1], T.dd[:, 128 * c:128 * c + 128], Op.min, ["dd%d" % c], ["fi%d" % c], apply_absolute_value=True)
+            n = 16 * c + 16
+            d, b, i = col("dd", 128 * c, n), sm1("nl", c), col("kk", 0, n)
+            op("vs", lambda e, d=d, b=b, i=i: V.tensor_scalar(d, i, b, None, Op.add) if e == "v" else S.activation(d, i, Act.Identity, bias=b), ["kk", "nl"], ["dd%d" % c])
+        for c in range(8):
+            red(sm1("fi", c), col("dd", 128 * c, 16 * c + 16), Op.min, ["dd%d" % c], ["fi%d" % c], apply_absolute_value=True)
         for t in range(4):
-            act(T.fg[:, 128 * t:128 * t + 128], T.fh[:, 320 * t:320 * t + 320].indirect(T.lw[:, 0:8]), ["fh%d" % t, "lw"], ["fg%d" % t])
+            times(blk("fg", t), blk("fh", t, 320).indirect(LW), [FH4[t], "lw"], ["fg%d" % t], 1.0)
         cp(T.fl[:], sm("fi"), ["fi%d" % c for c in range(8)], ["fl"])
-        if k == 2:
-            state_lists()
+        tt(sm("wn"), sm("fi"), sm("jw"), Op.is_equal, ["fi%d" % c for c in range(8)] + ["jw"], ["wn"])
+        ts(sm("xd"), LW, 4.0, Op.mult, ["lw"], ["xd"])
+        tt(sm("xe"), sm("xd"), sm("jd"), Op.subtract, ["xd", "jd"], ["xe"])
+        tt(sm("xd"), sm("xe"), sm("wn"), Op.mult, ["xe", "wn"], ["xd"])
+        tt(sm("xe"), sm("xd"), sm("jd"), Op.add, ["xd", "jd"], ["xe"])
         for t in range(4):
-            tt(T.nt[:, t:512:4], T.dh[:, 128 * t:128 * t + 128].indirect(T.fl[:]), T.fg[:, 128 * t:128 * t + 128], Op.add, ["dh%d" % t, "fl", "fg%d" % t], [N4[t]])
-        if k < 2:
-            state_lists()
-    quant(T.qv[:], T.sv[:], T.vi[:], ["vi"], ["qv"])
-    scatter_state()
+            ts(blk("xl", t, 8), sm("xe"), float(t), Op.add, ["xe"], ["xl%d" % t])
+        for t in range(4):
+            tt(T.nt[:, t:512:4], blk("dh", t).indirect(T.fl[:]), blk("fg", t), Op.add, [DH4[t], "fl", "fg%d" % t], [N4[t]])
+    for t in range(4):
+        cp(T.xt[:].indirect(blk("xl", t, 8)), T.nt[:, t:512:4], ["xl%d" % t, N4[t]], X4)
+    quant(T.qx[:], T.sx[:], col("xt", 0, 1280), X4, ["qx"])
     mm(PS[4][:, 0:320], T.qv[:], T.sv[:], T.qx[:], T.sx[:], ["qv", "qx"], ["#4"])
     dma("y", "do", T.oc[:], T.qx[:].bitcast(B8), ["qx"], [])
     for i in range(4):
-        dma("s" if i % 2 else "y", "do", T.osc[4 * i:4 * i + 4, :], T.sx[32 * i:32 * i + 4, :], ["qx"], [])
-    cp(T.yo[:], PS[4][:, 0:320], ["#4"], ["yo"])
+        dma("y", "do", T.osc[4 * i:4 * i + 4, :], T.sx[32 * i:32 * i + 4, :], ["qx"], [])
+    times(T.yo[:], PS[4][:, 0:320], ["#4"], ["yo"], 1.0)
     dma("s", "do", T.y[:], T.yo[:], ["yo"], [])
+    return ops
+
+
+def orders(ops):
+    wr, rd, out = {}, {}, []
+    for i, (q, _, reads, writes, kind, _, _) in enumerate(ops):
+        p = set()
+        for k in reads:
+            p.update(wr.get(k, []))
+            if k[0] == "#":
+                p.update(j for j in rd.get(k, []) if len(q + ops[j][0]) > 2 or ops[j][0] != q)
+        for k in writes:
+            if kind != "send":
+                p.update(wr.get(k, []) + rd.get(k, []))
+        for k in reads:
+            rd.setdefault(k, []).append(i)
+        for k in writes:
+            wr[k] = wr[k] + [i] if kind == "send" and k in wr else [i]
+            rd[k] = []
+        out.append(p)
+    return out
+
+
+def listed(text, ops):
+    out = []
+    for w in text.split():
+        a, e = w.rstrip("*"), 1 if w[-1] == "*" else 0
+        lo, hi = (a.split("-") + [a])[:2] if "-" in a else (a, a)
+        out += [(k, ops[k][0][e]) for k in range(int(lo), int(hi) + 1)]
+    return out
+
+
+def rank_program(g, core, T, topo):
+    if T.rank_of(core) is None:
+        return
+    ops = program(g, core, T, topo)
+    before = orders(ops)
+    Q = {"v": g.vector, "s": g.scalar, "t": g.tensor, "p": g, "y": g.sync}
+    known, tot, end, token = {q: {} for q in Q}, {}, {}, {}
+    for q, _, _, _, kind, sem, batch in ops:
+        if kind == "dma":
+            tot[sem] = tot.get(sem, 0) + 16
+            end[sem, batch] = tot[sem]
+        elif kind == "arrival":
+            tot[sem] = batch
+        elif kind == "send":
+            tot["ls"] = tot.get("ls", 0) + batch
+    for i, e in listed(ORDER_TEXT, ops) or [(k, ops[k][0][0]) for k in range(len(ops))]:
+        q, call, reads, writes, kind, sem, batch = ops[i]
+        if kind == "arrival":
+            token[i] = (sem, batch, {})
+            continue
+        want = {}
+        for j in before[i]:
+            if j not in token or (kind == "acc" and ops[j][0] == "t" and set(ops[j][3]) & set(writes)):
+                continue
+            s, val, snap = token[j]
+            if val > want.get(s, (0, None))[0]:
+                want[s] = (val, snap)
+        for s in sorted(want, key=lambda m: (-len(want[m][1]), m)):
+            val, snap = want[s]
+            if known[e].get(s, 0) < val:
+                Q[e].wait_ge(T.sem[s], val)
+                known[e][s] = val
+                for a, b in snap.items():
+                    known[e][a] = max(known[e].get(a, 0), b)
+        ins = call(e)
+        if kind == "dma":
+            ins.then_inc(T.sem[sem], 16)
+            token[i] = (sem, end[sem, batch], dict(known[e]))
+        elif kind != "send":
+            tot[e] = tot.get(e, 0) + 1
+            ins.then_inc(T.sem[e], 1)
+            token[i] = (e, tot[e], dict(known[e]))
     for sem in sorted(tot):
         if known["p"].get(sem, 0) < tot[sem]:
             g.wait_ge(T.sem[sem], tot[sem])

from concourse.mybir import dt, AluOpType as Op, AxisListType, ActivationFunctionType as Act

F32, BF, I32, U16, MXC, U8 = "float32", "bfloat16", "int32", "uint16", "float8_e4m3fn_x4", "uint8"
SCRATCH = {}
for _n, _w, _t in (
        ("xi", 1280, BF), ("ui", 512, BF), ("vi", 512, BF), ("mwi", 192, I32), ("mwf", 192, F32), ("cwi", 1280, I32), ("cwf", 1280, F32),
        ("wcs", 512, MXC), ("wps", 512, U8), ("wdc", 512, MXC), ("wdp", 512, U8),
        ("pi", 16, I32), ("pf", 32, F32), ("nat", 320, F32), ("nat512", 320, F32), ("ci", 160, I32), ("cj", 160, I32), ("cf", 192, F32), ("k20", 32, I32),
        ("tril", 128, BF), ("idb", 128, BF), ("mod", 128, BF), ("m8", 8, BF),
        ("l0", 4, U16), ("lr", 8, U16), ("lr7", 8, U16), ("ly", 20, U16), ("pk", 4, U16), ("la", 4, U16),
        ("zt", 512, BF), ("ce", 2048, BF), ("ca", 1536, BF), ("cb", 1536, BF),
        ("qe", 512, MXC), ("se", 512, U8), ("qa", 384, MXC), ("sa", 384, U8), ("qb", 384, MXC), ("sb", 384, U8),
        ("qu", 128, MXC), ("su", 128, U8), ("qv", 128, MXC), ("sv", 128, U8), ("fs", 192, F32),
        ("yb", 2560, F32), ("fw", 2880, F32), ("ox", 512, F32), ("o7", 128, F32), ("tt", 448, F32), ("of", 40, U16),
        ("rl", 128, F32), ("tl", 256, F32), ("lw", 16, U16), ("rle", 128, F32), ("te", 128, F32), ("ew", 32, I32),
        ("e1", 32, I32), ("e2", 32, I32), ("e3", 32, I32), ("ec", 32, I32), ("el", 8, U16), ("lc", 32, U16),
        ("rf", 768, F32), ("cp", 48, F32), ("ne", 32, F32), ("sk", 32, F32), ("pp", 32, F32), ("kk", 128, F32), ("dd", 1024, F32), ("fl", 8, U16),
        ("sg", 32, F32), ("xx", 32, F32), ("yy", 36, F32), ("qd", 8, I32), ("b1", 1536, BF), ("b2", 512, BF),
        ("qk", 384, MXC), ("sk1", 384, U8), ("ql", 128, MXC), ("sl", 128, U8), ("kt", 128, F32), ("eq", 128, F32), ("ofs", 8, U16), ("va", 128, F32),
        ("fh", 1280, BF), ("dh", 512, BF), ("fg", 512, F32), ("nt", 512, BF), ("qn", 128, MXC), ("sn", 128, U8), ("mt", 512, BF), ("ht", 512, BF),
        ("xt", 1792, BF), ("qx", 320, MXC), ("sx", 320, U8), ("xl", 32, U16), ("yo", 320, F32),
        ("qm0", 128, MXC), ("sm0", 128, U8), ("qm1", 128, MXC), ("sm1", 128, U8), ("qm2", 128, MXC), ("sm2", 128, U8),
        ("qh0", 128, MXC), ("sh0", 128, U8), ("qh1", 128, MXC), ("sh1", 128, U8), ("qh2", 128, MXC), ("sh2", 128, U8),
        ("mc0", 128, MXC), ("mp_0", 128, U8), ("mc1", 128, MXC), ("mp_1", 128, U8), ("hc0", 128, MXC), ("hp0", 128, U8), ("hc1", 128, MXC), ("hp1", 128, U8)):
    SCRATCH[_n] = ("sbuf", [128, _w], _t)
for _n in range(8):
    SCRATCH["p%d" % _n] = ("psum", [128, 512], F32)
SMALL = {n: 8 * k for k, n in enumerate(("jw", "jd", "sc", "nq", "dg", "kf", "lo", "kw", "dj", "t1", "t2", "rq", "fi", "wn", "xd", "nl", "xe"))}
SEMAPHORES = ["v", "s", "t", "p", "dx", "du", "dv", "dw", "da", "dc", "do", "aw", "am0", "am1", "ah0", "ah1", "ls"] + ["dm%d" % _n for _n in range(8)]
STEP = [1, 2, 3]
ORDER_TEXT = """
1 61 93 120 24 49 94 15 0 52 2 110 112 3-4 97 113 5-6 115 7 41 116 22 8 117-118 30 10 111 11-12 114 13-14 46 63 119 9 17-19 121 20-21 122 98 126
23 26 35 28 141 123 25 32 124 27 34 130 29 36 128 31 38 125 131 37 42 134 39 44 127 16 48 234 33 50 135 47 54 136 57 56 51 60 53 62 55 58 95 59
40 43 64 99 45 145 132 75 139 66 146 133 73 137 67 129 68-69 151 140 71-72 152 74 157 76 78-81 163 100 147 82 158 77 65 90 153 70 91 83-84 148
164 85-87 149 88 159 89 92 101 150 169 154 170 155 165 156 175 160 176 102 161 171 162 181 166 182 167 177 168 96 187 172 188 183 106 105 173
103 193 108 192 104 189 194 109 174 195 138 198 178 107 196 179-180 199 197 184-185 200 256 186 202 190 201 235 203 191 257 291 204 258 237 236*
238* 239 268 240 259 293 241 233 294 242-243 292 260-265 269 266-267 142 272 270 273 227 223 271 211 205-206 208 279 209 274 210 275 213 277 144
278 280-281 276 247 244 251* 245-246 248 249* 229 250 226 252 231 230 253 216 220 212 143 254-255 283 282 284-286 289 217 219 288 214 287 207
225 215 290 221 232 218 228 222 224 295 340 296 337 297 344 338 298 339 341 299-300 343 301 342 302 316 303 322 315 313* 304-305* 311 306* 314*
307 312 317 308-309 328 310 318 323 319-320 324 329 321* 330 325 332 326 331 327 333-336 345-364 368 365 369 366-367 370-371 392 372 389 390* 391
379-380 377 442 373-374 381 378* 382 376 388 375* 387 384 383 386 385 393 403 405-406 404 407 432 411 409 395 415* 410 413* 408 414* 412* 416 433
417 394 434 396 435-436 418 437 439 443 438 397 440 419 398 441 400 399 444 447* 445 446* 465 454 452 448 450 449 451 401 455 466 453 402 467-469
421 420 425* 422 424 423 426 471 427 462 428 472 475 463 456 429 457 473 458-461 476 470 430 464 477* 479 431 474* 480-481* 478* 482 525 483 524
484 529 526 485 527 530 486-487 528 488 531 489 503 490 509 502 493* 491-492* 498 501* 494 499-500* 495-496 504 497 515 505 510 506-507 511 516
508* 517 512 519 513 518 514 520-523 532-551 555 552 613 553-554 614 556 615 557 617 616 623 619 559 577 620 558 578 618 621 564 567 624 566 565
579 560-562 575-576 574 573 563* 572 568-571 622 580 625* 626 627* 628 590 629-630 591 632-634 592 635-636 631 593 582 594 583 581 598 597 584
602* 595 601* 596 599-600* 585 603 586-587 605 646 604 609* 606-607 610* 608 637 611* 638-642 612 643-644 663 645 664-670 684 671 690 682 672*
680* 673* 679 683* 681* 674* 685 675 686 696 687 647 676-678 688 691 697 689* 698 692 700 699 693 588 694 589 648 695 701-704 721 718 713-715 722
716 723 717 719 724 720 725-727 649 728-734 650 735 651 736 652 737 655 738 653 739 656 654 740 744 705 741 658 742 706 745 657 743 708 746 712*
765 748 707 747 766 711* 753 756 767 755 754 768 763 762 749 752* 751 764 750* 761 771 709 757 759-760 758 710 772 660* 662 770 769 661* 773 659
774 779 775 780 783 776 781 784 777-778 785 782 786-789 791-793 790 794* 795
"""


def program(g, core, T, topo):
    r = T.rank_of(core)
    N = len(T.cores)
    Q = {"v": g.vector, "s": g.scalar, "t": g.tensor, "p": g, "y": g.sync}
    ops = []

    def op(q, call, reads, writes, acc=False):
        ops.append([q, call, reads, writes, "acc" if acc else "op", None, 0])

    def dma(q, sem, out, in_, reads, writes, batch=0):
        ops.append([q, lambda _: Q[q].dma_start(out, in_), reads, writes, "dma", sem, batch])

    def send(pairs, dst, sem, reads):
        rid, pid, _ = topo.addr(dst)
        mask, n = topo.mask(core, dst), len(topo.engines(core, dst))
        for out, in_ in pairs:
            ops.append(["p", lambda _, out=out, in_=in_: g.remote_dma(out, in_, T.sem[sem], T.sem.ls, pid, rid, mask), reads, ["sent." + sem], "send", sem, n])

    def arrives(sem, src, writes):
        ops.append(["-", None, ["sent." + sem], writes, "arrival", sem, 2 * len(topo.engines(src, core))])

    V, S = g.vector, g.scalar
    B8 = dt.uint8

    def ts(out, in0, s1, op0, reads, writes, s2=None, op1=None):
        if op1 is None:
            op("v", lambda _: V.tensor_scalar(out, in0, s1, None, op0), reads, writes)
        else:
            op("v", lambda _: V.tensor_scalar(out, in0, s1, s2, op0, op1), reads, writes)

    def tt(out, a, b, o, reads, writes):
        op("v", lambda _: V.tensor_tensor(out, a, b, o), reads, writes)

    def cp(out, in_, reads, writes):
        op("v", lambda _: V.tensor_copy(out, in_), reads, writes)

    def tr(out, in_, reads, writes):
        op("v", lambda _: V.transpose(out, in_), reads, writes)

    def times(out, in_, reads, writes, scale, q="sv"):
        op(q, lambda e: S.activation(out, in_, Act.Copy, scale=scale) if e == "s" else V.tensor_scalar(out, in_, scale, None, Op.mult), reads, writes)

    def red(out, in_, o, reads, writes, **kw):
        op("v", lambda _: V.tensor_reduce(out, in_, AxisListType.X, o, **kw), reads, writes)

    def fill(ap, val, writes):
        op("v", lambda _: V.memset(ap, val), [], writes)

    def quant(q, s, t, reads, writes):
        op("v", lambda _: V.quantize_mx(q, s, t), reads, writes)

    def mm(out, l, ls, m, ms, reads, writes, start=True, stop=True):
        op("t", lambda _: g.tensor.matmul_mx(out, l, ls, m, ms, start, stop), reads, writes, acc=not start)

    def iota(out, pattern, base, cm, writes, flt):
        if flt:
            op("p", lambda _: g.iota(out, pattern, base, cm, allow_small_or_imprecise_dtypes=True), [], writes)
        else:
            op("p", lambda _: g.iota(out, pattern, base, cm), [], writes)

    def select(out, in_, pattern, cmp, fill_, base, cm, reads, writes):
        op("p", lambda _: g.affine_select(out, in_, pattern, cmp, fill_, base, cm), reads, writes)

    def col(name, k, n=1):
        return T[name][:, k:k + n]

    def sm(name, n=8):
        return T.fs[:, SMALL[name]:SMALL[name] + n]

    def sm1(name, k):
        return T.fs[:, SMALL[name] + k:SMALL[name] + k + 1]

    def blk(name, t, w=128):
        return T[name][:, w * t:w * t + w]

    PS = [T["p%d" % k] for k in range(8)]
    M4, H4, N4, X4 = [["%s%d" % (n, t) for t in range(4)] for n in "MHNX"]
    OX = ["ox%d" % k for k in range(8)]
    FWALL = ["fw%d" % s for s in range(8)]
    pf = lambda k: T.pf[:, k:k + 1]

    for m in range(8):
        for q in range(8):
            dma("ys"[q % 2], "dm%d" % m, T.mwi[16 * q:16 * q + 16, 24 * m:24 * m + 20], T.mp[16 * m:16 * m + 16, :], [], ["mwi%d.%d" % (m, q)])
        if m == 1:
            dma("y", "dx", T.xi[:], T.x[:], [], ["xi"])
    dma("y", "dw", T.wcs[:].bitcast(B8), T.wc[:], [], ["wcs"])
    dma("y", "dw", T.wps[:], T.ws[:], [], ["wps"])
    for i in range(16):
        dma("y", "da", T.cwi[i:128:16, :], T.ar[:], [], ["cwi%d" % i])
    for m in range(8):
        dma("y", "du", T.ui[:, 8 * m:8 * m + 8], T.u[:, 64 * m:64 * m + 8], [], ["ui%d" % m])
    dma("y", "du", T.ui[:, 64:512], T.u[:, 0:448], [], ["ui8"])
    dma("y", "dv", T.vi[:], T.v[:], [], ["vi"])

    iota(col("pi", 9), [[0, 1]], 0, 1, ["pi9"], False)
    iota(col("cf", 0, 20), [[2, 10], [0, 2]], 0, 0, ["cf0"], True)
    iota(col("cf", 32, 8), [[16, 4], [64, 2]], 0, 0, ["cf1"], True)
    iota(col("cf", 64, 64), [[32, 2], [64, 2], [1, 16]], 0, 0, ["cf4"], True)
    iota(T.nat[:], [[1, 320]], 0, 0, ["nat"], True)
    iota(T.zt[:], [[0, 512]], 0, 0, ["zt"], True)
    for b in range(4):
        select(blk("ce", b, 512), T.zt[:], [[-1, 512]], Op.not_equal, 1.0, b, 4, ["zt"], ["ce%d" % b])
    iota(col("ci", 0, 128), [[-1, 128]], 128, 1, ["cia"], False)
    iota(col("ci", 128, 8), [[-16, 8]], 0, 1, ["cib"], False)
    iota(col("cf", 56, 2), [[-16, 2]], 16, 0, ["cf3"], True)
    iota(T.k20[:], [[20, 4], [0, 8]], 0, 0, ["k20"], False)
    iota(T.nat512[:], [[512, 320]], 0, 0, ["nat512"], True)
    select(T.idb[:], blk("zt", 0), [[-1, 128]], Op.not_equal, 1.0, 0, 1, ["zt"], ["idb"])
    select(T.tril[:], blk("zt", 0), [[1, 128]], Op.is_ge, 1.0, 0, -1, ["zt"], ["tril"])
    for k, sh, an in ((0, 0, 15), (1, 4, 1), (2, 5, 3), (4, 0, 1), (5, 1, 1), (6, 2, 1), (7, 0, 7), (8, 3, 1)):
        ts(col("pi", k), col("pi", 9), sh, Op.logical_shift_right, ["pi9"], ["pi%d" % k], an, Op.bitwise_and)
    ts(col("pi", 3), col("pi", 9), 4, Op.logical_shift_right, ["pi9"], ["pi3"])
    cp(col("pf", 0, 10), col("pi", 0, 10), ["pi%d" % k for k in range(10)], ["pf"])
    fill(T.b2[:], 0.0, ["b2"])
    ts(T.ly[:], col("cf", 0, 20), pf(1), Op.add, ["cf0", "pf"], ["ly"])
    ts(pf(10), pf(1), 64.0, Op.mult, ["pf"], ["pf10"], pf(0), Op.add)
    ts(pf(11), pf(1), 16.0, Op.mult, ["pf"], ["pf11"])
    ts(pf(12), pf(2), 128.0, Op.mult, ["pf"], ["pf12"], pf(0), Op.add)
    tt(pf(13), pf(6), pf(4), Op.subtract, ["pf"], ["pf13"])
    ts(pf(15), pf(5), 4.0, Op.mult, ["pf"], ["pf15"], pf(4), Op.add)
    tt(pf(14), pf(13), pf(1), Op.mult, ["pf13", "pf"], ["pf14"])
    tt(pf(16), pf(15), pf(6), Op.add, ["pf15", "pf"], ["pf16"])
    ts(T.lr[:], col("cf", 32, 8), pf(12), Op.add, ["cf1", "pf12"], ["lr"])
    ts(pf(24), pf(2), 3.0, Op.is_lt, ["pf"], ["pf24"], 64.0, Op.mult)
    ts(pf(25), pf(24), pf(12), Op.add, ["pf24", "pf12"], ["pf25"])
    ts(T.lr7[:, 0:8:2], T.cf[:, 32:40:2], pf(12), Op.add, ["cf1", "pf12"], ["lr7_"])
    ts(T.lr7[:, 1:8:2], T.cf[:, 32:40:2], pf(25), Op.add, ["cf1", "pf25", "lr7_"], ["lr7"])
    ts(pf(26), pf(3), 7.0, Op.is_equal, ["pf"], ["pf26"], 128.0, Op.mult)
    ts(pf(17), pf(16), pf(4), Op.add, ["pf16", "pf14", "pf"], ["pf17"], pf(14), Op.add)
    ts(pf(23), pf(16), pf(6), Op.add, ["pf16", "pf14", "pf"], ["pf23"], pf(14), Op.subtract)
    ts(pf(18), pf(23), 16.0, Op.mult, ["pf23"], ["pf18"])
    ts(col("ox", 0, 64), col("cf", 64, 64), pf(11), Op.add, ["cf4", "pf11"], ["ox0"])
    ts(col("pk", 0), pf(17), 16.0, Op.mult, ["pf17", "pf26"], ["pk0"], pf(26), Op.add)
    ts(col("pk", 2, 2), col("cf", 0, 2), 0.0, Op.mult, ["cf0", "pf18"], ["pk1"], pf(18), Op.add)
    ts(T.l0[:], col("nat", 0, 4), 16.0, Op.mult, ["nat", "pf10"], ["l0"], pf(10), Op.add)
    fill(T.b1[:], 0.0, ["b1"])
    fill(T.ca[:], 0.0, ["ca"])
    fill(T.cb[:], 0.0, ["cb"])

    def step(s):
        if s == 7:
            cp(T.o7[:], col("fw", 320, 320).indirect(col("of", 24, 8)), ["fw7", "of6"], ["o7"])
            tr(col("tl", 128, 128), T.o7[:], ["o7"], ["tl7"])
            return
        lst, key = (T.l0[:], "l0") if s == 0 else (blk("of", s - 1, 4), "of%d" % (s - 1))
        cp(blk("ox", s + 1, 64), blk("fw", 8 - s, 320).indirect(lst), ["fw%d" % s, key], [OX[s + 1]])
        tr(blk("tt", s, 64), blk("ox", s + 1, 64), [OX[s + 1]], ["tt%d" % s])
        cp(col("of", 24, 8) if s == 6 else blk("of", s, 4), T.tt[:, 64 * s:64 * s + 64:8 if s == 6 else 16], ["tt%d" % s], ["of%d" % s])

    def places():
        cp(T.rl[:], col("ox", 64, 448).indirect(T.lr7[:]), OX[1:] + ["lr7"], ["rl"])
        tr(col("tl", 0, 128), T.rl[:], ["rl"], ["tl"])
        cp(T.lw[:], T.tl[:].indirect(col("pk", 0)), ["tl", "tl7", "pk0"], ["lw"])

    def decode(name, keys, w, q, s, key, scale, view=None):
        for t in range(4):
            mm(PS[t][:, 0:w], blk("qe", t), blk("se", t), q, s, ["qe", key], ["#%d" % t])
        for t in range(4):
            times(T[name][:, t:4 * w:4] if view else blk(name, t, w), PS[t][:, 0:w], ["#%d" % t], [keys[t]], scale)

    FH4, DH4 = ["fh%d" % t for t in range(4)], ["dh%d" % t for t in range(4)]
    LW = col("lw", 0, 8)

    for m in range(8):
        cp(col("mwf", 24 * m, 20), col("mwi", 24 * m, 20), ["mwi%d.%d" % (m, q) for q in range(8)], ["mwf%d" % m])
        times(blk("yb", m, 320), col("mwf", 24 * m, 20).indirect(T.ly[:]), ["mwf%d" % m, "ly"], ["yb%d" % m], 1.0)
        tr(blk("fw", 8 - m, 320), blk("yb", m, 320), ["yb%d" % m], ["fw%d" % m])
        step(m)
    quant(T.qx[:], T.sx[:], T.xi[:], ["xi"], ["qx"])
    quant(T.qe[:], T.se[:], T.ce[:], ["ce%d" % t for t in range(4)], ["qe"])
    decode("fh", FH4, 320, T.qx[:], T.sx[:], "qx", 0.5)
    places()

    for t in range(5):
        fill(sm1("sc", t), 32.0 ** -t, ["sc%d" % t])
    fill(sm1("sc", 5), 0.0, ["sc5"])
    ts(col("cj", 0, 128), col("ci", 0, 128), 15, Op.bitwise_and, ["cia"], ["cja"])
    ts(col("cj", 128, 8), col("ci", 128, 8), 4, Op.arith_shift_right, ["cib"], ["cjb"])
    ts(T.mod[:], col("cj", 0, 128), 0.0, Op.is_equal, ["cja"], ["mod"])
    ts(T.m8[:], col("cj", 128, 8), 0.0, Op.is_equal, ["cjb"], ["m8"])
    for t in range(3):
        ts(T.ca[:, 512 * t + t:512 * t + 512:4], T.mod[:], 0.0, Op.mult, ["mod", "ca"], ["ca.%d" % t], 32.0 ** t, Op.add)
        ts(T.cb[:, 512 * t + t:512 * t + 512:4], T.mod[:], 32.0 ** t, Op.mult, ["mod", "cb"], ["cb.%d" % t])
    quant(T.qa[:], T.sa[:], T.ca[:], ["ca"] + ["ca.%d" % t for t in range(3)], ["qa"])
    quant(T.qb[:], T.sb[:], T.cb[:], ["cb"] + ["cb.%d" % t for t in range(3)], ["qb"])
    quant(T.qu[:], T.su[:], T.ui[:], ["ui%d" % m for m in range(9)], ["qu"])
    quant(T.qv[:], T.sv[:], T.vi[:], ["vi"], ["qv"])
    ts(sm("jw"), col("nat", 0, 8), 16.0, Op.mult, ["nat", "pf"], ["jw"], pf(0), Op.add)
    ts(pf(19), pf(7), 2.0, Op.mult, ["pf"], ["pf19"])
    ts(pf(20), pf(8), -16.0, Op.mult, ["pf"], ["pf20"], 17.0, Op.add)
    ts(sm("jd"), sm("jw"), 4.0, Op.mult, ["jw"], ["jd"], 1280.0, Op.add)
    ts(col("yy", 32), pf(9), 1024.0, Op.mult, ["pf"], ["yyc"])
    ts(col("la", 0, 2), col("cf", 56, 2), pf(19), Op.add, ["cf3", "pf19"], ["la0"])
    tt(pf(21), pf(20), pf(19), Op.add, ["pf20", "pf19"], ["pf21"])
    ts(col("la", 2, 2), col("nat", 0, 2), 0.0, Op.mult, ["nat", "pf21"], ["la1"], pf(21), Op.add)
    cp(T.cwf[:], T.cwi[:], ["cwi%d" % i for i in range(16)], ["cwf"])
    ts(pf(22), pf(3), -327680.0, Op.mult, ["pf"], ["pf22"], 2621440.0, Op.add)

    heir = T.cores[(r - STEP[2]) % N]
    send([(T.wdp[:], T.wps[:])], heir, "aw", ["wps"])
    for k in range(3):
        donor, client = T.cores[(r + STEP[k]) % N], T.cores[(r - STEP[k]) % N]
        qm, sp, qh, sh = [T["%s%d" % (n, k)] for n in ("qm", "sm", "qh", "sh")]
        if k == 0:
            for t in range(4):
                times(T.mt[:, t:512:4], blk("fh", t, 320).indirect(LW), [FH4[t], "lw"], [M4[t]], 2.0)
        else:
            quant(T.qn[:], T.sn[:], T.nt[:], N4, ["qn"])
            decode("mt", M4, 128, T.qn[:], T.sn[:], "qn", 1.0, True)
        quant(qm[:], sp[:], T.mt[:], M4, ["qm%d" % k])
        mc, mp, mkey, wc, wp, wkeys = qm, sp, "qm%d" % k, T.wdc, T.wdp, ["wd"]
        hc, hp, hkey = qh, sh, "qh%d" % k
        if k < 2:
            send([(T["mc%d" % k][:].bitcast(B8), qm[:].bitcast(B8)), (T["mp_%d" % k][:], sp[:])], donor, "am%d" % k, ["qm%d" % k])
            mc, mp, mkey, wc, wp, wkeys = T["mc%d" % k], T["mp_%d" % k], "mc%d" % k, T.wcs, T.wps, ["wcs", "wps"]
            arrives("am%d" % k, client, [mkey])
        for b in range(4):
            mm(PS[b][:, 0:128], wc[:, 128 * b:128 * b + 128], wp[:, 128 * b:128 * b + 128], mc[:], mp[:], wkeys + [mkey], ["#%d" % b])
        for b in range(4):
            o, i = T.ht[:, b:512:4], PS[b][:, 0:128]
            op("vs", lambda e, o=o, i=i: V.tensor_scalar(o, i, 0.0, 0.03125, Op.max, Op.mult) if e == "v" else S.activation(o, i, Act.Relu, scale=0.03125), ["#%d" % b], [H4[b]])
        quant(qh[:], sh[:], T.ht[:], H4, ["qh%d" % k])
        if k < 2:
            send([(T["hc%d" % k][:].bitcast(B8), qh[:].bitcast(B8)), (T["hp%d" % k][:], sh[:])], client, "ah%d" % k, ["qh%d" % k])
            hc, hp, hkey = T["hc%d" % k], T["hp%d" % k], "hc%d" % k
            arrives("ah%d" % k, donor, [hkey])
            if k == 0:
                send([(T.wdc[:].bitcast(B8), T.wcs[:].bitcast(B8))], heir, "aw", ["wcs"])
                arrives("aw", T.cores[(r + STEP[2]) % N], ["wd"])
        cp(T.rle[:], T.ox[:].indirect(T.lr[:]), OX + ["lr"], ["rle"])
        tr(T.te[:], T.rle[:], ["rle"], ["te"])
        cp(T.ew[:], T.te[:].indirect(col("pk", 2, 2)), ["te", "pk1"], ["ew"])
        ts(T.e1[:], T.ew[:], 15, Op.bitwise_and, ["ew"], ["e1"])
        ts(T.e2[:], T.ew[:], 4, Op.logical_shift_right, ["ew"], ["e2"])
        cp(T.el[:], col("ew", 0, 8), ["ew"], ["el"])
        ts(T.e3[:], T.e1[:], 80.0, Op.mult, ["e1"], ["e3"])
        tt(T.ec[:], T.e2[:], T.k20[:], Op.add, ["e2", "k20"], ["ec"])
        tt(T.e1[:], T.e3[:], T.ec[:], Op.add, ["e3", "ec"], ["e1"])
        cp(T.lc[:], T.e1[:], ["e1"], ["lc"])
        times(T.rf[:, 4:768:6], T.nat[:].indirect(LW), ["nat", "lw"], ["rf4"], 1.0)
        op("s", lambda _: S.activation(T.rf[:, 5:768:6], T.nat[:].indirect(T.el[:]), Act.Identity, scale=1024.0, bias=pf(22)), ["nat", "el", "pf22"], ["rf5"])
        for q in range(4):
            times(T.rf[:, q:768:6], T.cwf[:].indirect(blk("lc", q, 8)), ["cwf", "lc"], ["rf%d" % q], 1.0)
        for m in range(8):
            dma("y", "dc", blk("cp", m, 6), T.rf[16 * m:16 * m + 1, 0:768], ["rf%d" % q for q in range(6)], ["cp%d" % m], k)
        C = ["cp%d" % m for m in range(8)]
        for q in range(4):
            tt(blk("ne", q, 8), T.cp[:, q:48:6], T.cp[:, 4:48:6], Op.not_equal, C, ["ne%d" % q])
            tt(blk("sk", q, 8), T.cp[:, q:48:6], T.cp[:, 5:48:6], Op.add, C, ["sk%d" % q])
        tt(T.pp[:], T.ne[:], T.sk[:], Op.mult, ["ne%d" % q for q in range(4)] + ["sk%d" % q for q in range(4)], ["pp"])
        if k:
            for t in range(4):
                cp(T.xt[:].indirect(blk("xl", t, 8)), T.nt[:, t:512:4], ["xl%d" % t, N4[t]], X4)
            quant(T.qx[:], T.sx[:], col("xt", 0, 1280), X4, ["qx"])
            decode("fh", FH4, 320, T.qx[:], T.sx[:], "qx", 0.5)
        for t in range(4):
            times(T.xt[:, t:1280:4], blk("fh", t, 320), [FH4[t]], [X4[t]], 2.0)
        mm(PS[4][:, 0:128], hc[:], hp[:], T.qu[:], T.su[:], [hkey, "qu"], ["#4"])
        ts(col("sg", 0, 16), PS[4][:, 0:16], 0.0, Op.is_gt, ["#4"], ["sg0"])
        ts(col("sg", 16, 16), PS[4][:, 0:16], 0.0, Op.is_le, ["#4"], ["sg1"])
        tt(T.xx[:], T.sg[:].indirect(col("la", 0, 2)), T.pp[:], Op.mult, ["sg0", "sg1", "la0", "pp"], ["xx"])
        tt(col("yy", 0, 32), T.sg[:].indirect(col("la", 2, 2)), T.xx[:], Op.mult, ["sg0", "sg1", "la1", "xx"], ["yy"])
        red(sm("rq", 1), col("yy", 0, 33), Op.max, ["yy", "yyc"], ["rq"])
        ts(col("qd", 0, 6), sm("sc", 6), sm("rq", 1), Op.mult, ["rq"] + ["sc%d" % t for t in range(6)], ["qd"])
        ts(sm("nq", 5), col("qd", 1, 5), -32.0, Op.mult, ["qd"], ["nq"])
        tt(sm("dg", 5), sm("nq", 5), col("qd", 0, 5), Op.add, ["nq", "qd"], ["dg"])
        for t in range(3):
            times(T.b1[:, t:512:4], T.idb[:], ["idb", "dg", "b1"], ["ba%d" % t], sm1("dg", 2 + t))
        quant(blk("qk", 0), blk("sk1", 0), col("b1", 0, 512), ["ba%d" % t for t in range(3)] + ["b1"], ["qk0"])
        for t in range(3):
            mm(PS[5][:, 0:128], blk("qa", t), blk("sa", t), blk("qk", 0), blk("sk1", 0), ["qa", "qk0"], ["#5"], t == 0, t == 2)
        for t in range(2):
            times(T.b1[:, 512 + t:1024:4], T.idb[:], ["idb", "dg", "b1"], ["bb%d" % t], sm1("dg", t))
        for t in range(3):
            times(T.b1[:, 1024 + t:1056:4], T.m8[:], ["m8", "dg", "b1"], ["bc%d" % t], sm1("dg", 2 + t))
        ts(sm("kf", 1), col("qd", 2), 1.0, Op.add, ["qd"], ["kf"])
        quant(blk("qk", 2), blk("sk1", 2), col("b1", 1024, 512), ["bc0", "bc1", "bc2", "b1"], ["qk2"])
        for t in range(3):
            mm(PS[7][:, 0:128], blk("qb", t), blk("sb", t), blk("qk", 2), blk("sk1", 2), ["qb", "qk2"], ["#7"], t == 0, t == 2)
        times(sm("kw"), PS[7][:, 0:8], ["#7"], ["kw"], 1.0)
        ts(T.kt[:], T.tril[:], sm("kf", 1), Op.mult, ["tril", "kf"], ["kt"], -1.0, Op.add)
        tt(T.eq[:], PS[5][:, 0:128], T.kt[:], Op.is_equal, ["#5", "kt"], ["eq"])
        red(sm("lo", 1), T.eq[:], Op.max, ["eq"], ["lo"])
        ts(T.b2[:, 0:32:4], T.m8[:], sm("lo", 1), Op.mult, ["m8", "lo", "b2"], ["b2a"])
        quant(T.ql[:], T.sl[:], T.b2[:], ["b2", "b2a"], ["ql"])
        mm(PS[4][:, 0:128], blk("qb", 0), blk("sb", 0), T.ql[:], T.sl[:], ["qb", "ql"], ["#4"])
        quant(blk("qk", 1), blk("sk1", 1), col("b1", 512, 512), ["bb0", "bb1", "b1"], ["qk1"])
        for t in range(2):
            mm(PS[6][:, 0:128], blk("qa", t), blk("sa", t), blk("qk", 1), blk("sk1", 1), ["qa", "qk1"], ["#6"], t == 0, t == 1)
        times(T.va[:], PS[6][:, 0:128], ["#6"], ["va"], 1.0)
        tt(sm("dj"), sm("jw"), sm("kw"), Op.subtract, ["jw", "kw"], ["dj"])
        tt(sm("t1"), PS[4][:, 0:8], sm("dj"), Op.mult, ["#4", "dj"], ["t1"])
        tt(sm("t2"), sm("t1"), sm("kw"), Op.add, ["t1", "kw"], ["t2"])
        cp(T.ofs[:], sm("t2"), ["t2"], ["ofs"])
        cp(T.fw[:].indirect(T.ofs[:]), T.va[:], ["ofs", "va"], FWALL)
        decode("dh", DH4, 128, hc[:], hp[:], hkey, 0.5)
        if k == 2:
            for m in range(8):
                dma("y", "do", T.fo[m:m + 1, :], T.fw[0:1, 320 * (8 - m):320 * (8 - m) + 320], ["fw%d" % m], [])
        for s in range(8):
            step(s)
        places()
        ts(sm("nl"), LW, -512.0, Op.mult, ["lw"], ["nl"])
        tt(T.kk[:], T.nat512[:].indirect(LW), col("nat", 0, 128), Op.add, ["nat512", "lw", "nat"], ["kk"])
        for c in range(8):
            n = 16 * c + 16
            d, b, i = col("dd", 128 * c, n), sm1("nl", c), col("kk", 0, n)
            op("vs", lambda e, d=d, b=b, i=i: V.tensor_scalar(d, i, b, None, Op.add) if e == "v" else S.activation(d, i, Act.Identity, bias=b), ["kk", "nl"], ["dd%d" % c])
        for c in range(8):
            red(sm1("fi", c), col("dd", 128 * c, 16 * c + 16), Op.min, ["dd%d" % c], ["fi%d" % c], apply_absolute_value=True)
        for t in range(4):
            times(blk("fg", t), blk("fh", t, 320).indirect(LW), [FH4[t], "lw"], ["fg%d" % t], 1.0)
        cp(T.fl[:], sm("fi"), ["fi%d" % c for c in range(8)], ["fl"])
        tt(sm("wn"), sm("fi"), sm("jw"), Op.is_equal, ["fi%d" % c for c in range(8)] + ["jw"], ["wn"])
        ts(sm("xd"), LW, 4.0, Op.mult, ["lw"], ["xd"])
        tt(sm("xe"), sm("xd"), sm("jd"), Op.subtract, ["xd", "jd"], ["xe"])
        tt(sm("xd"), sm("xe"), sm("wn"), Op.mult, ["xe", "wn"], ["xd"])
        tt(sm("xe"), sm("xd"), sm("jd"), Op.add, ["xd", "jd"], ["xe"])
        for t in range(4):
            ts(blk("xl", t, 8), sm("xe"), float(t), Op.add, ["xe"], ["xl%d" % t])
        for t in range(4):
            tt(T.nt[:, t:512:4], blk("dh", t).indirect(T.fl[:]), blk("fg", t), Op.add, [DH4[t], "fl", "fg%d" % t], [N4[t]])
    for t in range(4):
        cp(T.xt[:].indirect(blk("xl", t, 8)), T.nt[:, t:512:4], ["xl%d" % t, N4[t]], X4)
    quant(T.qx[:], T.sx[:], col("xt", 0, 1280), X4, ["qx"])
    mm(PS[4][:, 0:320], T.qv[:], T.sv[:], T.qx[:], T.sx[:], ["qv", "qx"], ["#4"])
    dma("y", "do", T.oc[:], T.qx[:].bitcast(B8), ["qx"], [])
    for i in range(4):
        dma("y", "do", T.osc[4 * i:4 * i + 4, :], T.sx[32 * i:32 * i + 4, :], ["qx"], [])
    times(T.yo[:], PS[4][:, 0:320], ["#4"], ["yo"], 1.0)
    dma("s", "do", T.y[:], T.yo[:], ["yo"], [])
    return ops


def orders(ops):
    wr, rd, out = {}, {}, []
    for i, (q, _, reads, writes, kind, _, _) in enumerate(ops):
        p = set()
        for k in reads:
            p.update(wr.get(k, []))
            if k[0] == "#":
                p.update(j for j in rd.get(k, []) if len(q + ops[j][0]) > 2 or ops[j][0] != q)
        for k in writes:
            if kind != "send":
                p.update(wr.get(k, []) + rd.get(k, []))
        for k in reads:
            rd.setdefault(k, []).append(i)
        for k in writes:
            wr[k] = wr[k] + [i] if kind == "send" and k in wr else [i]
            rd[k] = []
        out.append(p)
    return out


def listed(text, ops):
    out = []
    for w in text.split():
        a, e = w.rstrip("*"), 1 if w[-1] == "*" else 0
        lo, hi = (a.split("-") + [a])[:2] if "-" in a else (a, a)
        out += [(k, ops[k][0][e]) for k in range(int(lo), int(hi) + 1)]
    return out


def rank_program(g, core, T, topo):
    if T.rank_of(core) is None:
        return
    ops = program(g, core, T, topo)
    before = orders(ops)
    Q = {"v": g.vector, "s": g.scalar, "t": g.tensor, "p": g, "y": g.sync}
    known, tot, end, token = {q: {} for q in Q}, {}, {}, {}
    for q, _, _, _, kind, sem, batch in ops:
        if kind == "dma":
            tot[sem] = tot.get(sem, 0) + 16
            end[sem, batch] = tot[sem]
        elif kind == "arrival":
            tot[sem] = batch
        elif kind == "send":
            tot["ls"] = tot.get("ls", 0) + batch
    for i, e in listed(ORDER_TEXT, ops) or [(k, ops[k][0][0]) for k in range(len(ops))]:
        q, call, reads, writes, kind, sem, batch = ops[i]
        if kind == "arrival":
            token[i] = (sem, batch, {})
            continue
        want = {}
        for j in before[i]:
            if j not in token or (kind == "acc" and ops[j][0] == "t" and set(ops[j][3]) & set(writes)):
                continue
            s, val, snap = token[j]
            if val > want.get(s, (0, None))[0]:
                want[s] = (val, snap)
        for s in sorted(want, key=lambda m: (-len(want[m][1]), m)):
            val, snap = want[s]
            if known[e].get(s, 0) < val:
                Q[e].wait_ge(T.sem[s], val)
                known[e][s] = val
                for a, b in snap.items():
                    known[e][a] = max(known[e].get(a, 0), b)
        ins = call(e)
        if kind == "dma":
            ins.then_inc(T.sem[sem], 16)
            token[i] = (sem, end[sem, batch], dict(known[e]))
        elif kind != "send":
            tot[e] = tot.get(e, 0) + 1
            ins.then_inc(T.sem[e], 1)
            token[i] = (e, tot[e], dict(known[e]))
    for sem in sorted(tot):
        if known["p"].get(sem, 0) < tot[sem]:
            g.wait_ge(T.sem[sem], tot[sem])
